import numpy as np
import ml_dtypes


def mxq(x, axis, fmt="e4m3"):
    dtype, down = {"e4m3": (ml_dtypes.float8_e4m3fn, 7), "e5m2": (ml_dtypes.float8_e5m2, 14)}[fmt]
    v = np.moveaxis(np.asarray(x, np.float32).astype(ml_dtypes.bfloat16).astype(np.float64), axis, -1)
    blocks = v.reshape(v.shape[:-1] + (-1, 32))
    amax = np.abs(blocks).max(-1, keepdims=True)
    byte = np.maximum(np.where(amax > 0, np.frexp(amax)[1] - 1 + 127, 0) - down, 1)
    scale = np.exp2(byte - 127.0)
    codes = (blocks / scale).astype(np.float32).astype(dtype).astype(np.float64)
    return np.moveaxis((codes * scale).reshape(v.shape), -1, axis)


WIDE = False


def mx_kscale(k):
    if not WIDE:
        return np.ones(k)
    levels = np.array([10, -10, 5, -5, 0])
    if k % 512:
        return np.exp2(np.random.permutation(np.resize(levels, k // 32))).repeat(32)
    a = np.empty((k // 512, 16))
    for p in range(k // 512):
        a[p, :8] = np.random.permutation(np.resize(levels, 8))
        for g in range(8):
            far = levels[np.abs(levels - a[p, g]) >= 10]
            a[p, g + 8] = far[np.random.randint(len(far))]
    return np.exp2(a.ravel()).repeat(32)


def f64(x):
    return np.asarray(x).astype(np.float64)


def striped(idx):
    return np.tile(idx.reshape(-1, 16).T, (8, 1)).astype(np.uint16)


def unstriped(offs):
    return offs[:16].T.reshape(-1).astype(np.int64)


def pack_weight(w):
    k, n = w.shape
    w = f64(np.asarray(w, np.float32).astype(ml_dtypes.bfloat16)).reshape(k // 32, 32, n)
    amax = np.abs(w).max(1)
    byte = np.clip(np.where(amax > 0, np.frexp(amax)[1] - 1 + 127 - 7, 1), 1, 254)
    scaled = (w * np.exp2(127.0 - byte)[:, None, :]).reshape(k, n).astype(np.float32)
    words = np.ascontiguousarray(scaled.reshape(k // 512, 128, 4, n).transpose(0, 1, 3, 2)).astype(ml_dtypes.float8_e4m3fn).view(np.uint8)
    return words, np.ascontiguousarray(byte.astype(np.uint8).reshape(k // 512, 16, n))


def unpack_weight(words, scales):
    g, p, n, _ = words.shape
    vals = np.ascontiguousarray(words).view(ml_dtypes.float8_e4m3fn).astype(np.float64) * np.repeat(np.exp2(scales.astype(np.float64) - 127.0), 8, axis=1)[..., None]
    return vals.transpose(0, 1, 3, 2).reshape(g * 512, n)


def relu(v):
    return np.maximum(v, 0.0)


K, T, S, N = 1024, 2048, 512, 512


def setup_inputs():
    n = np.random.standard_normal
    s = mx_kscale(K)[:, None]
    c = mx_kscale(S)
    packed_xT = pack_weight(n((K, T)) * s)
    return {
        "x_words": packed_xT[0],
        "x_scales": packed_xT[1],
        "w1": (n((K, N)) / np.sqrt(K) / s).astype(np.float32),
        "wgt": (np.random.uniform(0.5, 1.0, (S, 1)) * c[:, None] / np.sqrt(S)).astype(np.float32),
        "inv": (np.random.uniform(0.6, 1.4, (S, 1)) / c[:, None]).astype(np.float32),
        "old": (n((N, N)) * 0.2 + np.eye(N)).astype(np.float32),
        "offs": striped(np.random.permutation(T)[:S]),
    }


def reference(x_words, x_scales, w1, wgt, inv, old, offs):
    xq = unpack_weight(x_words, x_scales)[:, unstriped(offs)]
    w1q = mxq(f64(w1), 0, "e4m3")
    y = relu(xq.T @ w1q)
    a = f64(wgt) * y
    vv = f64(inv) * y
    return 0.95 * f64(old) + 0.05 * ((mxq(a, 0, "e4m3").T @ mxq(vv, 0, "e4m3")))

@@ -1,0 +1,188 @@
+from contextlib import ExitStack
+
+import concourse.mybir as mybir
+
+K, T, S, N = 1024, 2048, 512, 512
+FLOPS = 2 * S * K * N + 2 * S * N * N
+
+F32 = mybir.dt.float32
+BF16 = mybir.dt.bfloat16
+I32 = mybir.dt.int32
+U32 = mybir.dt.uint32
+U16 = mybir.dt.uint16
+U8 = mybir.dt.uint8
+FP8X4 = mybir.dt.float8_e4m3fn_x4
+ALU = mybir.AluOpType
+ACT = mybir.ActivationFunctionType
+
+P = 128
+PACK = 4
+PASSES = K // (P * PACK)
+BLOCKS = N // P
+SCALAR_A = {1: "s", 2: "s", 3: "s"}
+WARM = 0
+LOADS = "x0 w00 x1 w01 w10 w11 w20 w21 w30 w31 o0 o1 o2 o3"
+ORDER = "w00s qw001 w01s qw012 w10s w11s qw102 w20s w21s qw202 w30s qw301 w31s qw312 y0 y1 y2 y3 k0 k1 k2 k3 v0 a0 qa002 a1 v1 qa102 a2 v2 qa202 a3 v3 qa312 qa301 o:corner,0,2,0,4 o:col2,0,2,4,6 o:row2,2,3,0,6 o:col3,0,3,6,8 o:y0,3,4,0,8"
+
+
+def tile_picked_ykfac_relu_p_kernel(tc, x_words, x_scales, w1, wgt, inv, old, offs, out):
+    nc = tc.nc
+    out_rows = out.rearrange("(i p) m -> p i m", p=P)
+    with ExitStack() as ctx:
+        keep = ctx.enter_context(tc.tile_pool(name="keep", bufs=1))
+        psum = ctx.enter_context(tc.psum_pool(name="psum", bufs=1))
+
+        offsets = keep.tile([P, S // 16], U16, name="offsets")
+        nc.sync.dma_start(offsets[:], offs)
+        all_scales = keep.tile([P, T], U8, name="all_scales", align_bytes=64)
+        nc.gpsimd.memset(all_scales[:].bitcast(I32), 0)
+        for q in range(4):
+            nc.scalar.dma_start(all_scales[32 * q : 32 * q + 8, :].bitcast(I32), x_scales[:, 4 * q : 4 * q + 4, :].bitcast(I32))
+        wgt_sb = keep.tile([P, 1, PACK], F32, name="wgt_sb")
+        inv_sb = keep.tile([P, 1, PACK], F32, name="inv_sb")
+        nc.scalar.dma_start(wgt_sb[:, 0, :], wgt.rearrange("(p j) o -> p (j o)", j=PACK))
+        nc.scalar.dma_start(inv_sb[:, 0, :], inv.rearrange("(p j) o -> p (j o)", j=PACK))
+
+        all_words = [keep.tile([P, T], I32, name=f"all_words{g}", align_bytes=64) for g in range(PASSES)]
+        w_view = w1.rearrange("(g p j) m -> g p j m", g=PASSES, j=PACK)
+        w_raw = {}
+        old_sb = keep.tile([P, BLOCKS, N], F32, name="old_sb")
+        for what in LOADS.split():
+            if what[0] == "x":
+                g = int(what[1])
+                nc.sync.dma_start(all_words[g][:], x_words[g].rearrange("p n r -> p (n r)").bitcast(I32))
+            elif what[0] == "w":
+                c, g = int(what[1]), int(what[2])
+                w_raw[c, g] = keep.tile([P, PACK, P], F32, name=f"w_raw{c}{g}")[:]
+                nc.sync.dma_start(w_raw[c, g], w_view[g][:, :, c * P : (c + 1) * P])
+            elif what[0] == "W":
+                c, g = int(what[1]), int(what[2])
+                both = keep.tile([P, PACK, 2 * P], F32, name=f"w_raw{c}{g}")
+                nc.sync.dma_start(both[:], w_view[g][:, :, c * P : (c + 2) * P])
+                w_raw[c, g] = both[:, :, 0:P]
+                w_raw[c + 1, g] = both[:, :, P : 2 * P]
+            else:
+                i = int(what[1])
+                nc.sync.dma_start(old_sb[:, i, :], old[i * P : (i + 1) * P, :])
+
+        a_factor = keep.tile([P, 1, PACK], F32, name="a_factor")
+        wgt_sign = keep.tile([P, 1, PACK], F32, name="wgt_sign")
+        v_factor = keep.tile([P, 1, PACK], F32, name="v_factor")
+        nc.scalar.activation(a_factor[:], wgt_sb[:], ACT.Abs)
+        nc.scalar.activation(wgt_sign[:], wgt_sb[:], ACT.Sign)
+
+        x_codes = [keep.tile([P, S], U32, name=f"x_codes{g}", align_bytes=64) for g in range(PASSES)]
+        picked_scales = keep.tile([P, S], U8, name="picked_scales", align_bytes=64)
+        x_planes = keep.tile([P, S], U8, name="x_planes", align_bytes=64)
+        nc.vector.tensor_copy(picked_scales[:], all_scales[:].indirect(offsets[:]))
+        nc.vector.tensor_copy(x_planes[:].rearrange("p (j m) -> p m j", j=PACK), picked_scales[:].rearrange("p (m j) -> p m j", j=PACK))
+        nc.vector.tensor_tensor(v_factor[:], inv_sb[:], wgt_sign[:], ALU.mult)
+        for g in range(PASSES):
+            nc.vector.tensor_copy(x_codes[g][:].rearrange("p (j m) -> p m j", j=PACK), all_words[g][:].bitcast(U32).indirect(offsets[:]))
+
+        kept = keep.tile([P, BLOCKS, N], F32, name="kept")
+        av_codes = [keep.tile([P, 2 * P], U32, name=f"av_codes{c}", align_bytes=64) for c in range(BLOCKS)]
+        av_scales = [keep.tile([P, 2 * P], U8, name=f"av_scales{c}", align_bytes=64) for c in range(BLOCKS)]
+        av_grouped = [keep.tile([P, 2, P, PACK], BF16, name=f"av_grouped{c}", align_bytes=64) for c in range(BLOCKS)]
+        w_grouped = [keep.tile([P, 2, P, PACK], BF16, name=f"w_grouped{c}", align_bytes=64) for c in range(BLOCKS)]
+        result = keep.tile([P, BLOCKS, N], F32, name="result")
+        w_codes = [keep.tile([P, PASSES * P], U32, name=f"w_codes{c}", align_bytes=64) for c in range(BLOCKS)]
+        w_scales = [keep.tile([P, PASSES * P], U8, name=f"w_scales{c}", align_bytes=64) for c in range(BLOCKS)]
+        y = {}
+
+        def scale_old(i):
+            nc.gpsimd.tensor_scalar(kept[:, i, :], old_sb[:, i, :], 0.95, 0.0, ALU.mult, ALU.add)
+
+        def interleave(engine, dst, src):
+            views = dst.rearrange("p (u i) j -> p u j i", i=4), src.rearrange("p j (u i) -> p u j i", i=4)
+            if engine == "s":
+                nc.scalar.copy(*views)
+            elif engine == "v":
+                nc.vector.tensor_copy(*views)
+            else:
+                nc.gpsimd.tensor_scalar(*views, 1.0, 0.0, ALU.mult, ALU.add)
+
+        def weights(c, g, engine):
+            interleave(engine, w_grouped[c][:, g], w_raw[c, g])
+
+        def warm():
+            idle = psum.tile([P, N], F32, name="corner")
+            for n in range(WARM):
+                nc.tensor.matmul_mx(
+                    out=idle[:],
+                    lhsT=w_codes[0][:, 0:P].bitcast(FP8X4),
+                    lhsT_scale=w_scales[0][:, 0:P],
+                    rhs=x_codes[0][:].bitcast(FP8X4),
+                    rhs_scale=x_planes[:],
+                    start=True,
+                    stop=True,
+                )
+
+        def first(c):
+            y[c] = psum.tile([P, PACK, P], F32, name=f"y{c}")
+            for j in range(PACK):
+                for g in range(PASSES):
+                    nc.tensor.matmul_mx(
+                        out=y[c][:, j, :],
+                        lhsT=x_codes[g][:, j * P : (j + 1) * P].bitcast(FP8X4),
+                        lhsT_scale=x_planes[4 * g : P, j * P : (j + 1) * P],
+                        rhs=w_codes[c][:, g * P : (g + 1) * P].bitcast(FP8X4),
+                        rhs_scale=w_scales[c][:, g * P : (g + 1) * P],
+                        start=(g == 0),
+                        stop=(g == PASSES - 1),
+                    )
+
+        def weigh(tag, c):
+            factor = a_factor if tag == "a" else v_factor
+            target = av_grouped[c][:, 0 if tag == "a" else 1]
+            if tag == "a" and c in SCALAR_A:
+                planar = keep.tile([P, PACK, P], BF16, name=f"a_planar{c}")
+                for j in range(PACK):
+                    nc.scalar.activation(planar[:, j, :], y[c][:, j, :], ACT.Relu, scale=factor[:, 0, j : j + 1])
+                interleave(SCALAR_A[c], target, planar[:])
+            else:
+                nc.vector.scalar_tensor_tensor(
+                    target, y[c][:].rearrange("p j m -> p m j"), 0.0, factor[:].to_broadcast([P, P, PACK]), ALU.max, ALU.mult
+                )
+
+        def quantize(tag, c, h0, h1):
+            codes, scales, source = (w_codes, w_scales, w_grouped) if tag == "w" else (av_codes, av_scales, av_grouped)
+            cols = slice(h0 * P, h1 * P)
+            nc.vector.quantize_mx(codes[c][:, cols].bitcast(FP8X4), scales[c][:, cols], source[c][:, h0:h1].rearrange("p h m j -> p (h m j)"))
+
+        def second(name, rows, cols):
+            width = cols.stop - cols.start
+            bank = psum.tile([P, len(rows), width], F32, name=name)
+            for n, i in enumerate(rows):
+                for at in range(cols.start, cols.stop, P):
+                    stop = min(at + P, cols.stop)
+                    piece = slice(P + at % P, P + at % P + stop - at)
+                    nc.tensor.matmul_mx(
+                        out=bank[:, n, at - cols.start : stop - cols.start],
+                        lhsT=av_codes[i][:, 0:P].bitcast(FP8X4),
+                        lhsT_scale=av_scales[i][:, 0:P],
+                        rhs=av_codes[at // P][:, piece].bitcast(FP8X4),
+                        rhs_scale=av_scales[at // P][:, piece],
+                        start=True,
+                        stop=True,
+                    )
+            span = slice(rows.start, rows.stop)
+            nc.vector.scalar_tensor_tensor(result[:, span, cols], bank[:], 0.05, kept[:, span, cols], ALU.mult, ALU.add)
+            nc.sync.dma_start(out_rows[:, span, cols], result[:, span, cols])
+
+        for what in ORDER.split():
+            if what[0] == "w":
+                weights(int(what[1]), int(what[2]), what[3])
+            elif what[0] == "h":
+                warm()
+            elif what[0] == "y":
+                first(int(what[1]))
+            elif what[0] in "av":
+                weigh(what[0], int(what[1]))
+            elif what[0] == "q":
+                quantize(what[1], int(what[2]), int(what[3]), int(what[4]))
+            elif what[0] == "k":
+                scale_old(int(what[1]))
+            else:
+                name, r0, r1, c0, c1 = what[2:].split(",")
+                second(name, range(int(r0), int(r1)), slice(int(c0) * 64, int(c1) * 64))

@@ -1,6 +1,7 @@
 from contextlib import ExitStack
 
 import concourse.mybir as mybir
+from concourse.masks import make_identity
 
 K, T, S, N = 1024, 2048, 512, 512
 FLOPS = 2 * S * K * N + 2 * S * N * N
@@ -17,12 +18,12 @@ ACT = mybir.ActivationFunctionType
 
 P = 128
 PACK = 4
+RUN = 8
+QUADRANT = 32
 PASSES = K // (P * PACK)
-BLOCKS = N // P
-SCALAR_A = {1: "s", 2: "s", 3: "s"}
-WARM = 0
-LOADS = "x0 w00 x1 w01 w10 w11 w20 w21 w30 w31 o0 o1 o2 o3"
-ORDER = "w00s qw001 w01s qw012 w10s w11s qw102 w20s w21s qw202 w30s qw301 w31s qw312 y0 y1 y2 y3 k0 k1 k2 k3 v0 a0 qa002 a1 v1 qa102 a2 v2 qa202 a3 v3 qa312 qa301 o:corner,0,2,0,4 o:col2,0,2,4,6 o:row2,2,3,0,6 o:col3,0,3,6,8 o:y0,3,4,0,8"
+CHUNKS = N // P
+A, V = 0, 1
+A_ON_SCALAR = (2, 3)
 
 
 def tile_picked_ykfac_relu_p_kernel(tc, x_words, x_scales, w1, wgt, inv, old, offs, out):
@@ -35,154 +36,168 @@ def tile_picked_ykfac_relu_p_kernel(tc, x_words, x_scales, w1, wgt, inv, old, of
         offsets = keep.tile([P, S // 16], U16, name="offsets")
         nc.sync.dma_start(offsets[:], offs)
         all_scales = keep.tile([P, T], U8, name="all_scales", align_bytes=64)
-        nc.gpsimd.memset(all_scales[:].bitcast(I32), 0)
-        for q in range(4):
-            nc.scalar.dma_start(all_scales[32 * q : 32 * q + 8, :].bitcast(I32), x_scales[:, 4 * q : 4 * q + 4, :].bitcast(I32))
-        wgt_sb = keep.tile([P, 1, PACK], F32, name="wgt_sb")
-        inv_sb = keep.tile([P, 1, PACK], F32, name="inv_sb")
-        nc.scalar.dma_start(wgt_sb[:, 0, :], wgt.rearrange("(p j) o -> p (j o)", j=PACK))
-        nc.scalar.dma_start(inv_sb[:, 0, :], inv.rearrange("(p j) o -> p (j o)", j=PACK))
+        nc.vector.memset(all_scales[:].bitcast(I32), 0)
+        factor_rows = keep.tile([P, P], F32, name="factor_rows")
+        identity = keep.tile([P, P], F32, name="identity")
+        nc.gpsimd.memset(factor_rows[:], 0.0)
 
         all_words = [keep.tile([P, T], I32, name=f"all_words{g}", align_bytes=64) for g in range(PASSES)]
         w_view = w1.rearrange("(g p j) m -> g p j m", g=PASSES, j=PACK)
         w_raw = {}
-        old_sb = keep.tile([P, BLOCKS, N], F32, name="old_sb")
-        for what in LOADS.split():
-            if what[0] == "x":
-                g = int(what[1])
-                nc.sync.dma_start(all_words[g][:], x_words[g].rearrange("p n r -> p (n r)").bitcast(I32))
-            elif what[0] == "w":
-                c, g = int(what[1]), int(what[2])
-                w_raw[c, g] = keep.tile([P, PACK, P], F32, name=f"w_raw{c}{g}")[:]
-                nc.sync.dma_start(w_raw[c, g], w_view[g][:, :, c * P : (c + 1) * P])
-            elif what[0] == "W":
-                c, g = int(what[1]), int(what[2])
-                both = keep.tile([P, PACK, 2 * P], F32, name=f"w_raw{c}{g}")
-                nc.sync.dma_start(both[:], w_view[g][:, :, c * P : (c + 2) * P])
-                w_raw[c, g] = both[:, :, 0:P]
-                w_raw[c + 1, g] = both[:, :, P : 2 * P]
-            else:
-                i = int(what[1])
-                nc.sync.dma_start(old_sb[:, i, :], old[i * P : (i + 1) * P, :])
+        old_sb = keep.tile([P, CHUNKS, N], F32, name="old_sb")
+
+        for n, factor in enumerate((wgt, inv)):
+            nc.gpsimd.dma_start(
+                factor_rows[PACK * n : PACK * (n + 1), :].rearrange("j (b r) -> j b r", r=RUN),
+                factor.rearrange("(b j r) o -> j b (r o)", j=PACK, r=RUN),
+            )
+
+        def load_words(g):
+            nc.sync.dma_start(all_words[g][:], x_words[g].rearrange("p n r -> p (n r)").bitcast(I32))
+
+        def load_scales(q, passes):
+            rows = slice(QUADRANT * q + PACK * passes.start, QUADRANT * q + PACK * passes.stop)
+            nc.sync.dma_start(all_scales[rows, :].bitcast(I32), x_scales[passes, PACK * q : PACK * (q + 1), :].bitcast(I32))
+
+        def load_weights(g, chunks):
+            raw = keep.tile([P, PACK, len(chunks) * P], F32, name=f"w_raw{chunks.start}{g}")
+            nc.sync.dma_start(raw[:], w_view[g][:, :, chunks.start * P : chunks.stop * P])
+            for n, c in enumerate(chunks):
+                w_raw[c, g] = raw[:, :, n * P : (n + 1) * P]
+
+        load_words(0)
+        for q in range(2):
+            load_scales(q, slice(0, PASSES))
+        for q in range(2, 4):
+            for g in range(PASSES):
+                load_scales(q, slice(g, g + 1))
+        load_words(1)
+        weight_loads = [(0, range(0, 2)), (1, range(0, 2)), (0, range(2, 4)), (1, range(2, 3)), (1, range(3, 4))]
+        for g, chunks in weight_loads:
+            load_weights(g, chunks)
+        for i in range(CHUNKS):
+            nc.sync.dma_start(old_sb[:, i, :], old[i * P : (i + 1) * P, :])
 
         a_factor = keep.tile([P, 1, PACK], F32, name="a_factor")
         wgt_sign = keep.tile([P, 1, PACK], F32, name="wgt_sign")
         v_factor = keep.tile([P, 1, PACK], F32, name="v_factor")
-        nc.scalar.activation(a_factor[:], wgt_sb[:], ACT.Abs)
-        nc.scalar.activation(wgt_sign[:], wgt_sb[:], ACT.Sign)
+        make_identity(nc, identity[:])
+        factors = psum.tile([P, P], F32, name="col3")
+        nc.tensor.transpose(factors[:], factor_rows[:], identity[:])
+        nc.scalar.activation(a_factor[:, 0, :], factors[:, 0:PACK], ACT.Abs)
+        nc.scalar.activation(wgt_sign[:, 0, :], factors[:, 0:PACK], ACT.Sign)
 
         x_codes = [keep.tile([P, S], U32, name=f"x_codes{g}", align_bytes=64) for g in range(PASSES)]
         picked_scales = keep.tile([P, S], U8, name="picked_scales", align_bytes=64)
         x_planes = keep.tile([P, S], U8, name="x_planes", align_bytes=64)
         nc.vector.tensor_copy(picked_scales[:], all_scales[:].indirect(offsets[:]))
-        nc.vector.tensor_copy(x_planes[:].rearrange("p (j m) -> p m j", j=PACK), picked_scales[:].rearrange("p (m j) -> p m j", j=PACK))
-        nc.vector.tensor_tensor(v_factor[:], inv_sb[:], wgt_sign[:], ALU.mult)
+        nc.vector.tensor_copy(
+            x_planes[:].bitcast(I32).rearrange("p (j b r) -> p j b r", j=PACK, r=RUN // 4),
+            picked_scales[:].bitcast(I32).rearrange("p (b j r) -> p j b r", j=PACK, r=RUN // 4),
+        )
+        nc.vector.tensor_tensor(v_factor[:, 0, :], factors[:, PACK : 2 * PACK], wgt_sign[:, 0, :], ALU.mult)
         for g in range(PASSES):
-            nc.vector.tensor_copy(x_codes[g][:].rearrange("p (j m) -> p m j", j=PACK), all_words[g][:].bitcast(U32).indirect(offsets[:]))
+            nc.vector.tensor_copy(
+                x_codes[g][:].rearrange("p (j b r) -> p b j r", j=PACK, r=RUN),
+                all_words[g][:].bitcast(U32).indirect(offsets[:]),
+            )
 
-        kept = keep.tile([P, BLOCKS, N], F32, name="kept")
-        av_codes = [keep.tile([P, 2 * P], U32, name=f"av_codes{c}", align_bytes=64) for c in range(BLOCKS)]
-        av_scales = [keep.tile([P, 2 * P], U8, name=f"av_scales{c}", align_bytes=64) for c in range(BLOCKS)]
-        av_grouped = [keep.tile([P, 2, P, PACK], BF16, name=f"av_grouped{c}", align_bytes=64) for c in range(BLOCKS)]
-        w_grouped = [keep.tile([P, 2, P, PACK], BF16, name=f"w_grouped{c}", align_bytes=64) for c in range(BLOCKS)]
-        result = keep.tile([P, BLOCKS, N], F32, name="result")
-        w_codes = [keep.tile([P, PASSES * P], U32, name=f"w_codes{c}", align_bytes=64) for c in range(BLOCKS)]
-        w_scales = [keep.tile([P, PASSES * P], U8, name=f"w_scales{c}", align_bytes=64) for c in range(BLOCKS)]
+        kept = keep.tile([P, CHUNKS, N], F32, name="kept")
+        av_codes = [keep.tile([P, 2 * P], U32, name=f"av_codes{c}", align_bytes=64) for c in range(CHUNKS)]
+        av_scales = [keep.tile([P, 2 * P], U8, name=f"av_scales{c}", align_bytes=64) for c in range(CHUNKS)]
+        av_grouped = [keep.tile([P, 2, P, PACK], BF16, name=f"av_grouped{c}", align_bytes=64) for c in range(CHUNKS)]
+        w_grouped = [keep.tile([P, PASSES, P, PACK], BF16, name=f"w_grouped{c}", align_bytes=64) for c in range(CHUNKS)]
+        result = keep.tile([P, CHUNKS, N], F32, name="result")
+        w_codes = [keep.tile([P, PASSES * P], U32, name=f"w_codes{c}", align_bytes=64) for c in range(CHUNKS)]
+        w_scales = [keep.tile([P, PASSES * P], U8, name=f"w_scales{c}", align_bytes=64) for c in range(CHUNKS)]
         y = {}
 
-        def scale_old(i):
-            nc.gpsimd.tensor_scalar(kept[:, i, :], old_sb[:, i, :], 0.95, 0.0, ALU.mult, ALU.add)
+        def interleave(copy, grouped, rows):
+            copy(grouped.rearrange("p (u i) j -> p u j i", i=4), rows.rearrange("p j (u i) -> p u j i", i=4))
 
-        def interleave(engine, dst, src):
-            views = dst.rearrange("p (u i) j -> p u j i", i=4), src.rearrange("p j (u i) -> p u j i", i=4)
-            if engine == "s":
-                nc.scalar.copy(*views)
-            elif engine == "v":
-                nc.vector.tensor_copy(*views)
-            else:
-                nc.gpsimd.tensor_scalar(*views, 1.0, 0.0, ALU.mult, ALU.add)
+        def quantize(codes, scales, grouped, first, last):
+            cols = slice(first * P, last * P)
+            nc.vector.quantize_mx(codes[:, cols].bitcast(FP8X4), scales[:, cols], grouped[:, first:last].rearrange("p h m j -> p (h m j)"))
 
-        def weights(c, g, engine):
-            interleave(engine, w_grouped[c][:, g], w_raw[c, g])
+        def quantize_weights(c, g):
+            interleave(nc.vector.tensor_copy if g == 0 else nc.scalar.copy, w_grouped[c][:, g], w_raw[c, g])
+            quantize(w_codes[c], w_scales[c], w_grouped[c], g, g + 1)
 
-        def warm():
-            idle = psum.tile([P, N], F32, name="corner")
-            for n in range(WARM):
-                nc.tensor.matmul_mx(
-                    out=idle[:],
-                    lhsT=w_codes[0][:, 0:P].bitcast(FP8X4),
-                    lhsT_scale=w_scales[0][:, 0:P],
-                    rhs=x_codes[0][:].bitcast(FP8X4),
-                    rhs_scale=x_planes[:],
-                    start=True,
-                    stop=True,
-                )
-
-        def first(c):
+        def first_product(c):
             y[c] = psum.tile([P, PACK, P], F32, name=f"y{c}")
             for j in range(PACK):
                 for g in range(PASSES):
                     nc.tensor.matmul_mx(
                         out=y[c][:, j, :],
                         lhsT=x_codes[g][:, j * P : (j + 1) * P].bitcast(FP8X4),
-                        lhsT_scale=x_planes[4 * g : P, j * P : (j + 1) * P],
+                        lhsT_scale=x_planes[PACK * g : P, j * P : (j + 1) * P],
                         rhs=w_codes[c][:, g * P : (g + 1) * P].bitcast(FP8X4),
                         rhs_scale=w_scales[c][:, g * P : (g + 1) * P],
                         start=(g == 0),
                         stop=(g == PASSES - 1),
                     )
 
-        def weigh(tag, c):
-            factor = a_factor if tag == "a" else v_factor
-            target = av_grouped[c][:, 0 if tag == "a" else 1]
-            if tag == "a" and c in SCALAR_A:
-                planar = keep.tile([P, PACK, P], BF16, name=f"a_planar{c}")
-                for j in range(PACK):
-                    nc.scalar.activation(planar[:, j, :], y[c][:, j, :], ACT.Relu, scale=factor[:, 0, j : j + 1])
-                interleave(SCALAR_A[c], target, planar[:])
-            else:
-                nc.vector.scalar_tensor_tensor(
-                    target, y[c][:].rearrange("p j m -> p m j"), 0.0, factor[:].to_broadcast([P, P, PACK]), ALU.max, ALU.mult
-                )
+        def weigh_on_vector(c, half, factor):
+            nc.vector.scalar_tensor_tensor(
+                av_grouped[c][:, half], y[c][:].rearrange("p j m -> p m j"), 0.0, factor[:].to_broadcast([P, P, PACK]), ALU.max, ALU.mult
+            )
 
-        def quantize(tag, c, h0, h1):
-            codes, scales, source = (w_codes, w_scales, w_grouped) if tag == "w" else (av_codes, av_scales, av_grouped)
-            cols = slice(h0 * P, h1 * P)
-            nc.vector.quantize_mx(codes[c][:, cols].bitcast(FP8X4), scales[c][:, cols], source[c][:, h0:h1].rearrange("p h m j -> p (h m j)"))
+        def weigh_a_on_scalar(c):
+            a_rows = keep.tile([P, PACK, P], BF16, name=f"a_rows{c}")
+            for j in range(PACK):
+                nc.scalar.activation(a_rows[:, j, :], y[c][:, j, :], ACT.Relu, scale=a_factor[:, 0, j : j + 1])
+            interleave(nc.scalar.copy, av_grouped[c][:, A], a_rows[:])
 
-        def second(name, rows, cols):
-            width = cols.stop - cols.start
-            bank = psum.tile([P, len(rows), width], F32, name=name)
-            for n, i in enumerate(rows):
-                for at in range(cols.start, cols.stop, P):
-                    stop = min(at + P, cols.stop)
-                    piece = slice(P + at % P, P + at % P + stop - at)
+        def scale_old(i):
+            nc.scalar.activation(kept[:, i, :], old_sb[:, i, :], ACT.Copy, scale=0.95)
+
+        def second_product(bank_name, row_chunks, col_chunks):
+            bank = psum.tile([P, len(row_chunks), len(col_chunks) * P], F32, name=bank_name)
+            for n, i in enumerate(row_chunks):
+                for place, m in enumerate(col_chunks):
                     nc.tensor.matmul_mx(
-                        out=bank[:, n, at - cols.start : stop - cols.start],
-                        lhsT=av_codes[i][:, 0:P].bitcast(FP8X4),
-                        lhsT_scale=av_scales[i][:, 0:P],
-                        rhs=av_codes[at // P][:, piece].bitcast(FP8X4),
-                        rhs_scale=av_scales[at // P][:, piece],
+                        out=bank[:, n, place * P : (place + 1) * P],
+                        lhsT=av_codes[i][:, A * P : (A + 1) * P].bitcast(FP8X4),
+                        lhsT_scale=av_scales[i][:, A * P : (A + 1) * P],
+                        rhs=av_codes[m][:, V * P : (V + 1) * P].bitcast(FP8X4),
+                        rhs_scale=av_scales[m][:, V * P : (V + 1) * P],
                         start=True,
                         stop=True,
                     )
-            span = slice(rows.start, rows.stop)
-            nc.vector.scalar_tensor_tensor(result[:, span, cols], bank[:], 0.05, kept[:, span, cols], ALU.mult, ALU.add)
-            nc.sync.dma_start(out_rows[:, span, cols], result[:, span, cols])
+            rows = slice(row_chunks.start, row_chunks.stop)
+            cols = slice(col_chunks.start * P, col_chunks.stop * P)
+            nc.vector.scalar_tensor_tensor(result[:, rows, cols], bank[:], 0.05, kept[:, rows, cols], ALU.mult, ALU.add)
+            nc.sync.dma_start(out_rows[:, rows, cols], result[:, rows, cols])
 
-        for what in ORDER.split():
-            if what[0] == "w":
-                weights(int(what[1]), int(what[2]), what[3])
-            elif what[0] == "h":
-                warm()
-            elif what[0] == "y":
-                first(int(what[1]))
-            elif what[0] in "av":
-                weigh(what[0], int(what[1]))
-            elif what[0] == "q":
-                quantize(what[1], int(what[2]), int(what[3]), int(what[4]))
-            elif what[0] == "k":
-                scale_old(int(what[1]))
+        for g, chunks in weight_loads:
+            for c in chunks:
+                quantize_weights(c, g)
+        for c in range(CHUNKS):
+            first_product(c)
+
+        for c in range(CHUNKS):
+            last = c == CHUNKS - 1
+            if c == 0:
+                scale_old(0)
+                scale_old(1)
+            if c in A_ON_SCALAR:
+                weigh_a_on_scalar(c)
+                if last:
+                    scale_old(2)
+                    scale_old(3)
+                weigh_on_vector(c, V, v_factor)
             else:
-                name, r0, r1, c0, c1 = what[2:].split(",")
-                second(name, range(int(r0), int(r1)), slice(int(c0) * 64, int(c1) * 64))
+                weigh_on_vector(c, V, v_factor)
+                weigh_on_vector(c, A, a_factor)
+            if last:
+                quantize(av_codes[c], av_scales[c], av_grouped[c], V, V + 1)
+                quantize(av_codes[c], av_scales[c], av_grouped[c], A, A + 1)
+            else:
+                quantize(av_codes[c], av_scales[c], av_grouped[c], A, V + 1)
+            if c == 1:
+                second_product("corner", range(0, 2), range(0, 2))
+
+        second_product("col2", range(0, 2), range(2, 3))
+        second_product("row2", range(2, 3), range(0, 3))
+        second_product("col3", range(0, 3), range(3, 4))
+        second_product("y0", range(3, 4), range(0, 4))

@@ -22,13 +22,11 @@ RUN = 8
 QUADRANT = 32
 PASSES = K // (P * PACK)
 CHUNKS = N // P
-A, V = 0, 1
-A_ON_SCALAR = (2, 3)
+A_ON_SCALAR = (0, 1)
 
 
 def tile_picked_ykfac_relu_p_kernel(tc, x_words, x_scales, w1, wgt, inv, old, offs, out):
     nc = tc.nc
-    out_rows = out.rearrange("(i p) m -> p i m", p=P)
     with ExitStack() as ctx:
         keep = ctx.enter_context(tc.tile_pool(name="keep", bufs=1))
         psum = ctx.enter_context(tc.psum_pool(name="psum", bufs=1))
@@ -44,7 +42,7 @@ def tile_picked_ykfac_relu_p_kernel(tc, x_words, x_scales, w1, wgt, inv, old, of
         all_words = [keep.tile([P, T], I32, name=f"all_words{g}", align_bytes=64) for g in range(PASSES)]
         w_view = w1.rearrange("(g p j) m -> g p j m", g=PASSES, j=PACK)
         w_raw = {}
-        old_sb = keep.tile([P, CHUNKS, N], F32, name="old_sb")
+        old_sb = [keep.tile([P, N], F32, name=f"old_sb{i}") for i in range(CHUNKS)]
 
         for n, factor in enumerate((wgt, inv)):
             nc.gpsimd.dma_start(
@@ -59,145 +57,183 @@ def tile_picked_ykfac_relu_p_kernel(tc, x_words, x_scales, w1, wgt, inv, old, of
             rows = slice(QUADRANT * q + PACK * passes.start, QUADRANT * q + PACK * passes.stop)
             nc.sync.dma_start(all_scales[rows, :].bitcast(I32), x_scales[passes, PACK * q : PACK * (q + 1), :].bitcast(I32))
 
-        def load_weights(g, chunks):
-            raw = keep.tile([P, PACK, len(chunks) * P], F32, name=f"w_raw{chunks.start}{g}")
-            nc.sync.dma_start(raw[:], w_view[g][:, :, chunks.start * P : chunks.stop * P])
-            for n, c in enumerate(chunks):
-                w_raw[c, g] = raw[:, :, n * P : (n + 1) * P]
+        def load_six_scales():
+            for q in range(2):
+                load_scales(q, slice(0, PASSES))
+            for q in range(2, 4):
+                for g in range(PASSES):
+                    load_scales(q, slice(g, g + 1))
 
-        load_words(0)
-        for q in range(2):
-            load_scales(q, slice(0, PASSES))
-        for q in range(2, 4):
-            for g in range(PASSES):
+        def load_pass_scales(g):
+            for q in range(4):
                 load_scales(q, slice(g, g + 1))
+
+        def load_weights(g, first, last):
+            raw = keep.tile([P, PACK, (last - first) * P], F32, name=f"w_raw{first}{g}")
+            nc.sync.dma_start(raw[:], w_view[g][:, :, first * P : last * P])
+            for c in range(first, last):
+                w_raw[c, g] = (raw, first)
+
+        def load_old(i):
+            nc.sync.dma_start(old_sb[i][:], old[i * P : (i + 1) * P, :])
+
+        load_weights(0, 0, 4)
+        load_six_scales()
+        load_words(0)
         load_words(1)
-        weight_loads = [(0, range(0, 2)), (1, range(0, 2)), (0, range(2, 4)), (1, range(2, 3)), (1, range(3, 4))]
-        for g, chunks in weight_loads:
-            load_weights(g, chunks)
+        for c in range(CHUNKS):
+            load_weights(1, c, c + 1)
         for i in range(CHUNKS):
-            nc.sync.dma_start(old_sb[:, i, :], old[i * P : (i + 1) * P, :])
+            load_old(i)
 
         a_factor = keep.tile([P, 1, PACK], F32, name="a_factor")
         wgt_sign = keep.tile([P, 1, PACK], F32, name="wgt_sign")
         v_factor = keep.tile([P, 1, PACK], F32, name="v_factor")
         make_identity(nc, identity[:])
-        factors = psum.tile([P, P], F32, name="col3")
+        factors = psum.tile([P, P], F32, name="row3")
         nc.tensor.transpose(factors[:], factor_rows[:], identity[:])
         nc.scalar.activation(a_factor[:, 0, :], factors[:, 0:PACK], ACT.Abs)
         nc.scalar.activation(wgt_sign[:, 0, :], factors[:, 0:PACK], ACT.Sign)
+        inv_sb = keep.tile([P, PACK], F32, name="inv_sb")
+        nc.scalar.copy(inv_sb[:], factors[:, PACK : 2 * PACK])
 
         x_codes = [keep.tile([P, S], U32, name=f"x_codes{g}", align_bytes=64) for g in range(PASSES)]
         picked_scales = keep.tile([P, S], U8, name="picked_scales", align_bytes=64)
         x_planes = keep.tile([P, S], U8, name="x_planes", align_bytes=64)
-        nc.vector.tensor_copy(picked_scales[:], all_scales[:].indirect(offsets[:]))
-        nc.vector.tensor_copy(
-            x_planes[:].bitcast(I32).rearrange("p (j b r) -> p j b r", j=PACK, r=RUN // 4),
-            picked_scales[:].bitcast(I32).rearrange("p (b j r) -> p j b r", j=PACK, r=RUN // 4),
-        )
-        nc.vector.tensor_tensor(v_factor[:, 0, :], factors[:, PACK : 2 * PACK], wgt_sign[:, 0, :], ALU.mult)
-        for g in range(PASSES):
+
+        def gather_scales():
+            nc.vector.tensor_copy(picked_scales[:], all_scales[:].indirect(offsets[:]))
+            nc.vector.tensor_copy(
+                x_planes[:].bitcast(I32).rearrange("p (j b r) -> p j b r", j=PACK, r=RUN // 4),
+                picked_scales[:].bitcast(I32).rearrange("p (b j r) -> p j b r", j=PACK, r=RUN // 4),
+            )
+
+        def make_v_factor():
+            nc.gpsimd.tensor_tensor(v_factor[:, 0, :], inv_sb[:], wgt_sign[:, 0, :], ALU.mult)
+
+        def gather_words(g):
             nc.vector.tensor_copy(
                 x_codes[g][:].rearrange("p (j b r) -> p b j r", j=PACK, r=RUN),
                 all_words[g][:].bitcast(U32).indirect(offsets[:]),
             )
 
+        def operand(name):
+            grouped = keep.tile([P, N, PACK], BF16, name=f"{name}_grouped", align_bytes=64)
+            codes = keep.tile([P, N], U32, name=f"{name}_codes", align_bytes=64)
+            scales = keep.tile([P, N], U8, name=f"{name}_scales", align_bytes=64)
+            return grouped, codes, scales
+
+        w_mx = [operand(f"w{g}") for g in range(PASSES)]
+        a_mx = operand("a")
+        v_mx = operand("v")
         kept = keep.tile([P, CHUNKS, N], F32, name="kept")
-        av_codes = [keep.tile([P, 2 * P], U32, name=f"av_codes{c}", align_bytes=64) for c in range(CHUNKS)]
-        av_scales = [keep.tile([P, 2 * P], U8, name=f"av_scales{c}", align_bytes=64) for c in range(CHUNKS)]
-        av_grouped = [keep.tile([P, 2, P, PACK], BF16, name=f"av_grouped{c}", align_bytes=64) for c in range(CHUNKS)]
-        w_grouped = [keep.tile([P, PASSES, P, PACK], BF16, name=f"w_grouped{c}", align_bytes=64) for c in range(CHUNKS)]
         result = keep.tile([P, CHUNKS, N], F32, name="result")
-        w_codes = [keep.tile([P, PASSES * P], U32, name=f"w_codes{c}", align_bytes=64) for c in range(CHUNKS)]
-        w_scales = [keep.tile([P, PASSES * P], U8, name=f"w_scales{c}", align_bytes=64) for c in range(CHUNKS)]
-        y = {}
+        y = [psum.tile([P, PACK, P], F32, name=f"y{c}") for c in range(CHUNKS)]
+
+        def columns(first, last):
+            return slice(first * P, last * P)
 
         def interleave(copy, grouped, rows):
             copy(grouped.rearrange("p (u i) j -> p u j i", i=4), rows.rearrange("p j (u i) -> p u j i", i=4))
 
-        def quantize(codes, scales, grouped, first, last):
-            cols = slice(first * P, last * P)
-            nc.vector.quantize_mx(codes[:, cols].bitcast(FP8X4), scales[:, cols], grouped[:, first:last].rearrange("p h m j -> p (h m j)"))
+        def cast(copy, g, first, last):
+            raw, start = w_raw[first, g]
+            interleave(copy, w_mx[g][0][:, columns(first, last)], raw[:, :, columns(first - start, last - start)])
 
-        def quantize_weights(c, g):
-            interleave(nc.vector.tensor_copy if g == 0 else nc.scalar.copy, w_grouped[c][:, g], w_raw[c, g])
-            quantize(w_codes[c], w_scales[c], w_grouped[c], g, g + 1)
+        def quantize(mx, first, last):
+            grouped, codes, scales = mx
+            cols = columns(first, last)
+            nc.vector.quantize_mx(codes[:, cols].bitcast(FP8X4), scales[:, cols], grouped[:, cols].rearrange("p m j -> p (m j)"))
 
-        def first_product(c):
-            y[c] = psum.tile([P, PACK, P], F32, name=f"y{c}")
+        def first_product(c, g):
             for j in range(PACK):
-                for g in range(PASSES):
-                    nc.tensor.matmul_mx(
-                        out=y[c][:, j, :],
-                        lhsT=x_codes[g][:, j * P : (j + 1) * P].bitcast(FP8X4),
-                        lhsT_scale=x_planes[PACK * g : P, j * P : (j + 1) * P],
-                        rhs=w_codes[c][:, g * P : (g + 1) * P].bitcast(FP8X4),
-                        rhs_scale=w_scales[c][:, g * P : (g + 1) * P],
-                        start=(g == 0),
-                        stop=(g == PASSES - 1),
-                    )
+                nc.tensor.matmul_mx(
+                    out=y[c][:, j, :],
+                    lhsT=x_codes[g][:, columns(j, j + 1)].bitcast(FP8X4),
+                    lhsT_scale=x_planes[PACK * g : P, columns(j, j + 1)],
+                    rhs=w_mx[g][1][:, columns(c, c + 1)].bitcast(FP8X4),
+                    rhs_scale=w_mx[g][2][:, columns(c, c + 1)],
+                    start=(g == 0 and j == 0),
+                    stop=(g == PASSES - 1 and j == PACK - 1),
+                )
 
-        def weigh_on_vector(c, half, factor):
+        def weigh_on_vector(c, mx, factor):
             nc.vector.scalar_tensor_tensor(
-                av_grouped[c][:, half], y[c][:].rearrange("p j m -> p m j"), 0.0, factor[:].to_broadcast([P, P, PACK]), ALU.max, ALU.mult
+                mx[0][:, columns(c, c + 1)], y[c][:].rearrange("p j m -> p m j"), 0.0, factor[:].to_broadcast([P, P, PACK]), ALU.max, ALU.mult
             )
 
-        def weigh_a_on_scalar(c):
-            a_rows = keep.tile([P, PACK, P], BF16, name=f"a_rows{c}")
+        a_rows = [keep.tile([P, PACK, P], BF16, name=f"a_rows{c}") for c in range(CHUNKS)]
+
+        def weigh_a_rows(c):
             for j in range(PACK):
-                nc.scalar.activation(a_rows[:, j, :], y[c][:, j, :], ACT.Relu, scale=a_factor[:, 0, j : j + 1])
-            interleave(nc.scalar.copy, av_grouped[c][:, A], a_rows[:])
+                nc.scalar.activation(a_rows[c][:, j, :], y[c][:, j, :], ACT.Relu, scale=a_factor[:, 0, j : j + 1])
+
+        def interleave_a(copy, c):
+            interleave(copy, a_mx[0][:, columns(c, c + 1)], a_rows[c][:])
+
+        out_rows = out.rearrange("(i p) m -> p i m", p=P)
+        banks = {}
 
         def scale_old(i):
-            nc.scalar.activation(kept[:, i, :], old_sb[:, i, :], ACT.Copy, scale=0.95)
+            nc.scalar.activation(kept[:, i, :], old_sb[i][:], ACT.Copy, scale=0.95)
 
-        def second_product(bank_name, row_chunks, col_chunks):
-            bank = psum.tile([P, len(row_chunks), len(col_chunks) * P], F32, name=bank_name)
-            for n, i in enumerate(row_chunks):
-                for place, m in enumerate(col_chunks):
-                    nc.tensor.matmul_mx(
-                        out=bank[:, n, place * P : (place + 1) * P],
-                        lhsT=av_codes[i][:, A * P : (A + 1) * P].bitcast(FP8X4),
-                        lhsT_scale=av_scales[i][:, A * P : (A + 1) * P],
-                        rhs=av_codes[m][:, V * P : (V + 1) * P].bitcast(FP8X4),
-                        rhs_scale=av_scales[m][:, V * P : (V + 1) * P],
-                        start=True,
-                        stop=True,
-                    )
-            rows = slice(row_chunks.start, row_chunks.stop)
-            cols = slice(col_chunks.start * P, col_chunks.stop * P)
-            nc.vector.scalar_tensor_tensor(result[:, rows, cols], bank[:], 0.05, kept[:, rows, cols], ALU.mult, ALU.add)
-            nc.sync.dma_start(out_rows[:, rows, cols], result[:, rows, cols])
+        def scale_old_gpsimd(i):
+            nc.gpsimd.tensor_scalar(kept[:, i, :], old_sb[i][:], 0.95, 0.0, ALU.mult, ALU.add)
 
-        for g, chunks in weight_loads:
-            for c in chunks:
-                quantize_weights(c, g)
+        def second_product(name, rows, cols):
+            banks[rows, cols] = psum.tile([P, rows[1] - rows[0], (cols[1] - cols[0]) * P], F32, name=name)
+            for i in range(*rows):
+                nc.tensor.matmul_mx(
+                    out=banks[rows, cols][:, i - rows[0], :],
+                    lhsT=a_mx[1][:, columns(i, i + 1)].bitcast(FP8X4),
+                    lhsT_scale=a_mx[2][:, columns(i, i + 1)],
+                    rhs=v_mx[1][:, columns(*cols)].bitcast(FP8X4),
+                    rhs_scale=v_mx[2][:, columns(*cols)],
+                    start=True,
+                    stop=True,
+                )
+
+        def average(rows, cols):
+            part = (slice(None), slice(*rows), columns(*cols))
+            nc.vector.scalar_tensor_tensor(result[part], banks[rows, cols][:], 0.05, kept[part], ALU.mult, ALU.add)
+            nc.sync.dma_start(out_rows[part], result[part])
+
+        on_gpsimd = nc.gpsimd.tensor_copy
+        on_vector, on_scalar = nc.vector.tensor_copy, nc.scalar.copy
+        cast(on_vector, 0, 0, 2)
+        cast(on_scalar, 0, 2, 4)
+        make_v_factor()
+        gather_scales()
+        quantize(w_mx[0], 0, 2)
+        quantize(w_mx[0], 2, 4)
+        gather_words(0)
         for c in range(CHUNKS):
-            first_product(c)
-
+            first_product(c, 0)
+        gather_words(1)
         for c in range(CHUNKS):
-            last = c == CHUNKS - 1
-            if c == 0:
-                scale_old(0)
-                scale_old(1)
+            cast(on_scalar, 1, c, c + 1)
+            quantize(w_mx[1], c, c + 1)
+            first_product(c, 1)
+        for c in range(CHUNKS):
+            weigh_on_vector(c, v_mx, v_factor)
             if c in A_ON_SCALAR:
-                weigh_a_on_scalar(c)
-                if last:
-                    scale_old(2)
-                    scale_old(3)
-                weigh_on_vector(c, V, v_factor)
+                weigh_a_rows(c)
+                interleave_a(on_scalar, c)
             else:
-                weigh_on_vector(c, V, v_factor)
-                weigh_on_vector(c, A, a_factor)
-            if last:
-                quantize(av_codes[c], av_scales[c], av_grouped[c], V, V + 1)
-                quantize(av_codes[c], av_scales[c], av_grouped[c], A, A + 1)
-            else:
-                quantize(av_codes[c], av_scales[c], av_grouped[c], A, V + 1)
-            if c == 1:
-                second_product("corner", range(0, 2), range(0, 2))
-
-        second_product("col2", range(0, 2), range(2, 3))
-        second_product("row2", range(2, 3), range(0, 3))
-        second_product("col3", range(0, 3), range(3, 4))
-        second_product("y0", range(3, 4), range(0, 4))
+                weigh_on_vector(c, a_mx, a_factor)
+        quantize(v_mx, 0, 2)
+        quantize(a_mx, 0, 1)
+        second_product("corner", (0, 1), (0, 2))
+        quantize(v_mx, 2, 4)
+        second_product("right", (0, 1), (2, 4))
+        quantize(a_mx, 1, 2)
+        second_product("row1", (1, 2), (0, 4))
+        quantize(a_mx, 2, 4)
+        second_product("y0", (2, 3), (0, 4))
+        second_product("row3", (3, 4), (0, 4))
+        for i in range(CHUNKS):
+            scale_old_gpsimd(i)
+        average((0, 1), (0, 2))
+        average((0, 1), (2, 4))
+        for i in (1, 2, 3):
+            average((i, i + 1), (0, 4))

@@ -232,7 +232,7 @@ def tile_picked_ykfac_relu_p_kernel(tc, x_words, x_scales, w1, wgt, inv, old, of
         second_product("y0", (2, 3), (0, 4))
         second_product("row3", (3, 4), (0, 4))
         for i in range(CHUNKS):
-            scale_old_gpsimd(i)
+            scale_old(i)
         average((0, 1), (0, 2))
         average((0, 1), (2, 4))
         for i in (1, 2, 3):

@@ -1,7 +1,6 @@
 from contextlib import ExitStack
 
 import concourse.mybir as mybir
-from concourse.masks import make_identity
 
 K, T, S, N = 1024, 2048, 512, 512
 FLOPS = 2 * S * K * N + 2 * S * N * N
@@ -18,11 +17,11 @@ ACT = mybir.ActivationFunctionType
 
 P = 128
 PACK = 4
-RUN = 8
 QUADRANT = 32
 PASSES = K // (P * PACK)
 CHUNKS = N // P
-A_ON_SCALAR = (0, 1)
+HALF = CHUNKS // 2
+ROWS = (1, 0, 3, 2)
 
 
 def tile_picked_ykfac_relu_p_kernel(tc, x_words, x_scales, w1, wgt, inv, old, offs, out):
@@ -31,121 +30,88 @@ def tile_picked_ykfac_relu_p_kernel(tc, x_words, x_scales, w1, wgt, inv, old, of
         keep = ctx.enter_context(tc.tile_pool(name="keep", bufs=1))
         psum = ctx.enter_context(tc.psum_pool(name="psum", bufs=1))
 
+        def columns(first, last):
+            return slice(first * P, last * P)
+
         offsets = keep.tile([P, S // 16], U16, name="offsets")
         nc.sync.dma_start(offsets[:], offs)
         all_scales = keep.tile([P, T], U8, name="all_scales", align_bytes=64)
         nc.vector.memset(all_scales[:].bitcast(I32), 0)
-        factor_rows = keep.tile([P, P], F32, name="factor_rows")
-        identity = keep.tile([P, P], F32, name="identity")
-        nc.gpsimd.memset(factor_rows[:], 0.0)
 
-        all_words = [keep.tile([P, T], I32, name=f"all_words{g}", align_bytes=64) for g in range(PASSES)]
         w_view = w1.rearrange("(g p j) m -> g p j m", g=PASSES, j=PACK)
         w_raw = {}
-        old_sb = [keep.tile([P, N], F32, name=f"old_sb{i}") for i in range(CHUNKS)]
-
-        for n, factor in enumerate((wgt, inv)):
-            nc.gpsimd.dma_start(
-                factor_rows[PACK * n : PACK * (n + 1), :].rearrange("j (b r) -> j b r", r=RUN),
-                factor.rearrange("(b j r) o -> j b (r o)", j=PACK, r=RUN),
-            )
-
-        def load_words(g):
-            nc.sync.dma_start(all_words[g][:], x_words[g].rearrange("p n r -> p (n r)").bitcast(I32))
-
-        def load_scales(q, passes):
-            rows = slice(QUADRANT * q + PACK * passes.start, QUADRANT * q + PACK * passes.stop)
-            nc.sync.dma_start(all_scales[rows, :].bitcast(I32), x_scales[passes, PACK * q : PACK * (q + 1), :].bitcast(I32))
-
-        def load_six_scales():
-            for q in range(2):
-                load_scales(q, slice(0, PASSES))
-            for q in range(2, 4):
-                for g in range(PASSES):
-                    load_scales(q, slice(g, g + 1))
-
-        def load_pass_scales(g):
-            for q in range(4):
-                load_scales(q, slice(g, g + 1))
 
         def load_weights(g, first, last):
-            raw = keep.tile([P, PACK, (last - first) * P], F32, name=f"w_raw{first}{g}")
-            nc.sync.dma_start(raw[:], w_view[g][:, :, first * P : last * P])
+            raw = keep.tile([P, PACK, (last - first) * P], F32, name=f"w_raw{g}{first}")
+            nc.sync.dma_start(raw[:], w_view[g][:, :, columns(first, last)])
             for c in range(first, last):
-                w_raw[c, g] = (raw, first)
+                w_raw[g, c] = raw[:, :, columns(c - first, c - first + 1)]
 
-        def load_old(i):
-            nc.sync.dma_start(old_sb[i][:], old[i * P : (i + 1) * P, :])
-
-        load_weights(0, 0, 4)
-        load_six_scales()
-        load_words(0)
-        load_words(1)
+        pass0 = keep.tile([P, PACK, N], F32, name="pass0")
+        nc.sync.dma_start(pass0[:], w_view[0])
+        for q in range(P // QUADRANT):
+            rows = slice(QUADRANT * q, QUADRANT * q + PACK * PASSES)
+            nc.sync.dma_start(all_scales[rows, :].bitcast(I32), x_scales[:, PACK * q : PACK * (q + 1), :].bitcast(I32))
+        all_words = [keep.tile([P, T], I32, name=f"all_words{g}", align_bytes=64) for g in range(PASSES)]
+        wgt_sb = keep.tile([P, PACK], F32, name="wgt_sb")
+        inv_sb = keep.tile([P, PACK], F32, name="inv_sb")
+        nc.sync.dma_start(all_words[0][:], x_words[0].rearrange("p n r -> p (n r)").bitcast(I32))
+        nc.sync.dma_start(wgt_sb[:], wgt.rearrange("(p j) o -> p (j o)", j=PACK))
+        nc.sync.dma_start(inv_sb[:], inv.rearrange("(p j) o -> p (j o)", j=PACK))
+        nc.sync.dma_start(all_words[1][:], x_words[1].rearrange("p n r -> p (n r)").bitcast(I32))
         for c in range(CHUNKS):
             load_weights(1, c, c + 1)
-        for i in range(CHUNKS):
-            load_old(i)
+        old_sb = [keep.tile([P, N], F32, name=f"old_sb{i}") for i in range(CHUNKS)]
+        for i in ROWS:
+            nc.sync.dma_start(old_sb[i][:], old[columns(i, i + 1), :])
 
         a_factor = keep.tile([P, 1, PACK], F32, name="a_factor")
-        wgt_sign = keep.tile([P, 1, PACK], F32, name="wgt_sign")
+        wgt_sign = keep.tile([P, PACK], F32, name="wgt_sign")
         v_factor = keep.tile([P, 1, PACK], F32, name="v_factor")
-        make_identity(nc, identity[:])
-        factors = psum.tile([P, P], F32, name="row3")
-        nc.tensor.transpose(factors[:], factor_rows[:], identity[:])
-        nc.scalar.activation(a_factor[:, 0, :], factors[:, 0:PACK], ACT.Abs)
-        nc.scalar.activation(wgt_sign[:, 0, :], factors[:, 0:PACK], ACT.Sign)
-        inv_sb = keep.tile([P, PACK], F32, name="inv_sb")
-        nc.scalar.copy(inv_sb[:], factors[:, PACK : 2 * PACK])
-
-        x_codes = [keep.tile([P, S], U32, name=f"x_codes{g}", align_bytes=64) for g in range(PASSES)]
-        picked_scales = keep.tile([P, S], U8, name="picked_scales", align_bytes=64)
-        x_planes = keep.tile([P, S], U8, name="x_planes", align_bytes=64)
-
-        def gather_scales():
-            nc.vector.tensor_copy(picked_scales[:], all_scales[:].indirect(offsets[:]))
-            nc.vector.tensor_copy(
-                x_planes[:].bitcast(I32).rearrange("p (j b r) -> p j b r", j=PACK, r=RUN // 4),
-                picked_scales[:].bitcast(I32).rearrange("p (b j r) -> p j b r", j=PACK, r=RUN // 4),
-            )
-
-        def make_v_factor():
-            nc.gpsimd.tensor_tensor(v_factor[:, 0, :], inv_sb[:], wgt_sign[:, 0, :], ALU.mult)
-
-        def gather_words(g):
-            nc.vector.tensor_copy(
-                x_codes[g][:].rearrange("p (j b r) -> p b j r", j=PACK, r=RUN),
-                all_words[g][:].bitcast(U32).indirect(offsets[:]),
-            )
+        nc.scalar.activation(a_factor[:, 0, :], wgt_sb[:], ACT.Abs)
+        nc.scalar.activation(wgt_sign[:], wgt_sb[:], ACT.Sign)
+        nc.vector.tensor_tensor(v_factor[:, 0, :], inv_sb[:], wgt_sign[:], ALU.mult)
 
         def operand(name):
             grouped = keep.tile([P, N, PACK], BF16, name=f"{name}_grouped", align_bytes=64)
-            codes = keep.tile([P, N], U32, name=f"{name}_codes", align_bytes=64)
+            codes = keep.tile([P, N], U32, name="all_scales" if name == "w0" else f"{name}_codes", align_bytes=64)
             scales = keep.tile([P, N], U8, name=f"{name}_scales", align_bytes=64)
             return grouped, codes, scales
 
         w_mx = [operand(f"w{g}") for g in range(PASSES)]
         a_mx = operand("a")
         v_mx = operand("v")
-        kept = keep.tile([P, CHUNKS, N], F32, name="kept")
-        result = keep.tile([P, CHUNKS, N], F32, name="result")
+        x_codes = [keep.tile([P, S], U32, name=f"x_codes{g}", align_bytes=64) for g in range(PASSES)]
+        x_planes = keep.tile([P, S], U8, name="x_planes", align_bytes=64)
         y = [psum.tile([P, PACK, P], F32, name=f"y{c}") for c in range(CHUNKS)]
-
-        def columns(first, last):
-            return slice(first * P, last * P)
+        a_rows = [keep.tile([P, PACK, P], BF16, name=f"a_rows{c}") for c in range(CHUNKS)]
+        result = keep.tile([P, CHUNKS, N], F32, name="result")
+        out_rows = out.rearrange("(i p) m -> p i m", p=P)
+        kept = {}
+        banks = {}
 
         def interleave(copy, grouped, rows):
             copy(grouped.rearrange("p (u i) j -> p u j i", i=4), rows.rearrange("p j (u i) -> p u j i", i=4))
 
-        def cast(copy, g, first, last):
-            raw, start = w_raw[first, g]
-            interleave(copy, w_mx[g][0][:, columns(first, last)], raw[:, :, columns(first - start, last - start)])
+        def cast(copy, g, c):
+            interleave(copy, w_mx[g][0][:, columns(c, c + 1)], w_raw[g, c])
+
+        def cast_half(copy, first):
+            cols = columns(first, first + HALF)
+            interleave(copy, w_mx[0][0][:, cols], pass0[:, :, cols])
 
         def quantize(mx, first, last):
             grouped, codes, scales = mx
             cols = columns(first, last)
             nc.vector.quantize_mx(codes[:, cols].bitcast(FP8X4), scales[:, cols], grouped[:, cols].rearrange("p m j -> p (m j)"))
 
-        def first_product(c, g):
+        def gather_scales():
+            nc.vector.tensor_copy(x_planes[:].rearrange("p (j m) -> p m j", j=PACK), all_scales[:].indirect(offsets[:]))
+
+        def gather_words(g):
+            nc.vector.tensor_copy(x_codes[g][:].rearrange("p (j m) -> p m j", j=PACK), all_words[g][:].bitcast(U32).indirect(offsets[:]))
+
+        def first_product(g, c):
             for j in range(PACK):
                 nc.tensor.matmul_mx(
                     out=y[c][:, j, :],
@@ -157,83 +123,72 @@ def tile_picked_ykfac_relu_p_kernel(tc, x_words, x_scales, w1, wgt, inv, old, of
                     stop=(g == PASSES - 1 and j == PACK - 1),
                 )
 
-        def weigh_on_vector(c, mx, factor):
+        def weigh_on_vector(mx, factor, c):
             nc.vector.scalar_tensor_tensor(
                 mx[0][:, columns(c, c + 1)], y[c][:].rearrange("p j m -> p m j"), 0.0, factor[:].to_broadcast([P, P, PACK]), ALU.max, ALU.mult
             )
-
-        a_rows = [keep.tile([P, PACK, P], BF16, name=f"a_rows{c}") for c in range(CHUNKS)]
 
         def weigh_a_rows(c):
             for j in range(PACK):
                 nc.scalar.activation(a_rows[c][:, j, :], y[c][:, j, :], ACT.Relu, scale=a_factor[:, 0, j : j + 1])
 
-        def interleave_a(copy, c):
-            interleave(copy, a_mx[0][:, columns(c, c + 1)], a_rows[c][:])
+        def interleave_a(c):
+            interleave(nc.scalar.copy, a_mx[0][:, columns(c, c + 1)], a_rows[c][:])
 
-        out_rows = out.rearrange("(i p) m -> p i m", p=P)
-        banks = {}
+        def scale_old(rows, name):
+            space = keep.tile([P, len(rows), N], F32, name=name)
+            for n, i in enumerate(rows):
+                kept[i] = space[:, n : n + 1, :]
+                nc.scalar.activation(space[:, n, :], old_sb[i][:], ACT.Copy, scale=0.95)
 
-        def scale_old(i):
-            nc.scalar.activation(kept[:, i, :], old_sb[i][:], ACT.Copy, scale=0.95)
+        def second_product(name, i, cols):
+            banks[i, cols] = psum.tile([P, 1, (cols[1] - cols[0]) * P], F32, name=name)
+            nc.tensor.matmul_mx(
+                out=banks[i, cols][:, 0, :],
+                lhsT=a_mx[1][:, columns(i, i + 1)].bitcast(FP8X4),
+                lhsT_scale=a_mx[2][:, columns(i, i + 1)],
+                rhs=v_mx[1][:, columns(*cols)].bitcast(FP8X4),
+                rhs_scale=v_mx[2][:, columns(*cols)],
+                start=True,
+                stop=True,
+            )
 
-        def scale_old_gpsimd(i):
-            nc.gpsimd.tensor_scalar(kept[:, i, :], old_sb[i][:], 0.95, 0.0, ALU.mult, ALU.add)
-
-        def second_product(name, rows, cols):
-            banks[rows, cols] = psum.tile([P, rows[1] - rows[0], (cols[1] - cols[0]) * P], F32, name=name)
-            for i in range(*rows):
-                nc.tensor.matmul_mx(
-                    out=banks[rows, cols][:, i - rows[0], :],
-                    lhsT=a_mx[1][:, columns(i, i + 1)].bitcast(FP8X4),
-                    lhsT_scale=a_mx[2][:, columns(i, i + 1)],
-                    rhs=v_mx[1][:, columns(*cols)].bitcast(FP8X4),
-                    rhs_scale=v_mx[2][:, columns(*cols)],
-                    start=True,
-                    stop=True,
-                )
-
-        def average(rows, cols):
-            part = (slice(None), slice(*rows), columns(*cols))
-            nc.vector.scalar_tensor_tensor(result[part], banks[rows, cols][:], 0.05, kept[part], ALU.mult, ALU.add)
+        def average(i, cols):
+            part = (slice(None), slice(i, i + 1), columns(*cols))
+            nc.vector.scalar_tensor_tensor(result[part], banks[i, cols][:], 0.05, kept[i][:, :, columns(*cols)], ALU.mult, ALU.add)
             nc.sync.dma_start(out_rows[part], result[part])
 
-        on_gpsimd = nc.gpsimd.tensor_copy
         on_vector, on_scalar = nc.vector.tensor_copy, nc.scalar.copy
-        cast(on_vector, 0, 0, 2)
-        cast(on_scalar, 0, 2, 4)
-        make_v_factor()
+        cast_half(on_vector, 0)
+        cast_half(on_scalar, HALF)
         gather_scales()
-        quantize(w_mx[0], 0, 2)
-        quantize(w_mx[0], 2, 4)
+        quantize(w_mx[0], 0, HALF)
+        quantize(w_mx[0], HALF, CHUNKS)
         gather_words(0)
         for c in range(CHUNKS):
-            first_product(c, 0)
+            first_product(0, c)
         gather_words(1)
         for c in range(CHUNKS):
-            cast(on_scalar, 1, c, c + 1)
+            cast(on_scalar, 1, c)
             quantize(w_mx[1], c, c + 1)
-            first_product(c, 1)
+            first_product(1, c)
         for c in range(CHUNKS):
-            weigh_on_vector(c, v_mx, v_factor)
-            if c in A_ON_SCALAR:
+            weigh_on_vector(v_mx, v_factor, c)
+            if c % 2 == 0:
                 weigh_a_rows(c)
-                interleave_a(on_scalar, c)
+                interleave_a(c)
             else:
-                weigh_on_vector(c, a_mx, a_factor)
-        quantize(v_mx, 0, 2)
-        quantize(a_mx, 0, 1)
-        second_product("corner", (0, 1), (0, 2))
-        quantize(v_mx, 2, 4)
-        second_product("right", (0, 1), (2, 4))
-        quantize(a_mx, 1, 2)
-        second_product("row1", (1, 2), (0, 4))
-        quantize(a_mx, 2, 4)
-        second_product("y0", (2, 3), (0, 4))
-        second_product("row3", (3, 4), (0, 4))
-        for i in range(CHUNKS):
-            scale_old(i)
-        average((0, 1), (0, 2))
-        average((0, 1), (2, 4))
-        for i in (1, 2, 3):
-            average((i, i + 1), (0, 4))
+                weigh_on_vector(a_mx, a_factor, c)
+        scale_old(ROWS, "kept")
+        quantize(v_mx, 0, HALF)
+        quantize(a_mx, ROWS[0], ROWS[0] + 1)
+        second_product("left", ROWS[0], (0, HALF))
+        quantize(v_mx, HALF, CHUNKS)
+        second_product("right", ROWS[0], (HALF, CHUNKS))
+        for i in ROWS[1:]:
+            quantize(a_mx, i, i + 1)
+            second_product(f"y{i}", i, (0, CHUNKS))
+        average(ROWS[0], (0, HALF))
+        average(ROWS[0], (HALF, CHUNKS))
+        for i in ROWS[1:]:
+            average(i, (0, CHUNKS))

@@ -41,14 +41,15 @@ def tile_picked_ykfac_relu_p_kernel(tc, x_words, x_scales, w1, wgt, inv, old, of
         w_view = w1.rearrange("(g p j) m -> g p j m", g=PASSES, j=PACK)
         w_raw = {}
 
-        def load_weights(g, first, last):
+        def load_weights(g, first, last, queue=nc.sync):
             raw = keep.tile([P, PACK, (last - first) * P], F32, name=f"w_raw{g}{first}")
-            nc.sync.dma_start(raw[:], w_view[g][:, :, columns(first, last)])
+            queue.dma_start(raw[:], w_view[g][:, :, columns(first, last)])
             for c in range(first, last):
                 w_raw[g, c] = raw[:, :, columns(c - first, c - first + 1)]
 
         pass0 = keep.tile([P, PACK, N], F32, name="pass0")
         nc.sync.dma_start(pass0[:], w_view[0])
+        load_weights(1, 0, 1, nc.scalar)
         for q in range(P // QUADRANT):
             rows = slice(QUADRANT * q, QUADRANT * q + PACK * PASSES)
             nc.sync.dma_start(all_scales[rows, :].bitcast(I32), x_scales[:, PACK * q : PACK * (q + 1), :].bitcast(I32))
@@ -59,7 +60,7 @@ def tile_picked_ykfac_relu_p_kernel(tc, x_words, x_scales, w1, wgt, inv, old, of
         nc.sync.dma_start(wgt_sb[:], wgt.rearrange("(p j) o -> p (j o)", j=PACK))
         nc.sync.dma_start(inv_sb[:], inv.rearrange("(p j) o -> p (j o)", j=PACK))
         nc.sync.dma_start(all_words[1][:], x_words[1].rearrange("p n r -> p (n r)").bitcast(I32))
-        for c in range(CHUNKS):
+        for c in range(1, CHUNKS):
             load_weights(1, c, c + 1)
         old_sb = [keep.tile([P, N], F32, name=f"old_sb{i}") for i in range(CHUNKS)]
         for i in ROWS:
@@ -73,7 +74,7 @@ def tile_picked_ykfac_relu_p_kernel(tc, x_words, x_scales, w1, wgt, inv, old, of
         nc.vector.tensor_tensor(v_factor[:, 0, :], inv_sb[:], wgt_sign[:], ALU.mult)
 
         def operand(name):
-            grouped = keep.tile([P, N, PACK], BF16, name=f"{name}_grouped", align_bytes=64)
+            grouped = {}
             codes = keep.tile([P, N], U32, name="all_scales" if name == "w0" else f"{name}_codes", align_bytes=64)
             scales = keep.tile([P, N], U8, name=f"{name}_scales", align_bytes=64)
             return grouped, codes, scales
@@ -84,26 +85,35 @@ def tile_picked_ykfac_relu_p_kernel(tc, x_words, x_scales, w1, wgt, inv, old, of
         x_codes = [keep.tile([P, S], U32, name=f"x_codes{g}", align_bytes=64) for g in range(PASSES)]
         x_planes = keep.tile([P, S], U8, name="x_planes", align_bytes=64)
         y = [psum.tile([P, PACK, P], F32, name=f"y{c}") for c in range(CHUNKS)]
-        a_rows = [keep.tile([P, PACK, P], BF16, name=f"a_rows{c}") for c in range(CHUNKS)]
+        a_rows = {}
         result = keep.tile([P, CHUNKS, N], F32, name="result")
         out_rows = out.rearrange("(i p) m -> p i m", p=P)
         kept = {}
         banks = {}
 
+        def stage(mx, first, last, name):
+            space = keep.tile([P, (last - first) * P, PACK], BF16, name=name, align_bytes=64)
+            for c in range(first, last):
+                mx[0][c] = (space, first)
+
+        def staged(mx, first, last):
+            space, start = mx[0][first]
+            return space[:, columns(first - start, last - start)]
+
         def interleave(copy, grouped, rows):
             copy(grouped.rearrange("p (u i) j -> p u j i", i=4), rows.rearrange("p j (u i) -> p u j i", i=4))
 
         def cast(copy, g, c):
-            interleave(copy, w_mx[g][0][:, columns(c, c + 1)], w_raw[g, c])
+            interleave(copy, staged(w_mx[g], c, c + 1), w_raw[g, c])
 
         def cast_half(copy, first):
             cols = columns(first, first + HALF)
-            interleave(copy, w_mx[0][0][:, cols], pass0[:, :, cols])
+            interleave(copy, staged(w_mx[0], first, first + HALF), pass0[:, :, cols])
 
         def quantize(mx, first, last):
-            grouped, codes, scales = mx
+            codes, scales = mx[1:]
             cols = columns(first, last)
-            nc.vector.quantize_mx(codes[:, cols].bitcast(FP8X4), scales[:, cols], grouped[:, cols].rearrange("p m j -> p (m j)"))
+            nc.vector.quantize_mx(codes[:, cols].bitcast(FP8X4), scales[:, cols], staged(mx, first, last).rearrange("p m j -> p (m j)"))
 
         def gather_scales():
             nc.vector.tensor_copy(x_planes[:].rearrange("p (j m) -> p m j", j=PACK), all_scales[:].indirect(offsets[:]))
@@ -125,15 +135,16 @@ def tile_picked_ykfac_relu_p_kernel(tc, x_words, x_scales, w1, wgt, inv, old, of
 
         def weigh_on_vector(mx, factor, c):
             nc.vector.scalar_tensor_tensor(
-                mx[0][:, columns(c, c + 1)], y[c][:].rearrange("p j m -> p m j"), 0.0, factor[:].to_broadcast([P, P, PACK]), ALU.max, ALU.mult
+                staged(mx, c, c + 1), y[c][:].rearrange("p j m -> p m j"), 0.0, factor[:].to_broadcast([P, P, PACK]), ALU.max, ALU.mult
             )
 
         def weigh_a_rows(c):
+            a_rows[c] = keep.tile([P, PACK, P], BF16, name="w_raw12" if c == 0 else f"a_rows{c}")
             for j in range(PACK):
                 nc.scalar.activation(a_rows[c][:, j, :], y[c][:, j, :], ACT.Relu, scale=a_factor[:, 0, j : j + 1])
 
         def interleave_a(c):
-            interleave(nc.scalar.copy, a_mx[0][:, columns(c, c + 1)], a_rows[c][:])
+            interleave(nc.scalar.copy, staged(a_mx, c, c + 1), a_rows[c][:])
 
         def scale_old(rows, name):
             space = keep.tile([P, len(rows), N], F32, name=name)
@@ -159,6 +170,11 @@ def tile_picked_ykfac_relu_p_kernel(tc, x_words, x_scales, w1, wgt, inv, old, of
             nc.sync.dma_start(out_rows[part], result[part])
 
         on_vector, on_scalar = nc.vector.tensor_copy, nc.scalar.copy
+        stage(w_mx[0], 0, CHUNKS, "w0_grouped")
+        for c in range(CHUNKS):
+            stage(w_mx[1], c, c + 1, f"w1_grouped{c}")
+        stage(a_mx, 0, CHUNKS, "a_grouped")
+        stage(v_mx, HALF, CHUNKS, "v_late")
         cast_half(on_vector, 0)
         cast_half(on_scalar, HALF)
         gather_scales()
@@ -172,6 +188,7 @@ def tile_picked_ykfac_relu_p_kernel(tc, x_words, x_scales, w1, wgt, inv, old, of
             cast(on_scalar, 1, c)
             quantize(w_mx[1], c, c + 1)
             first_product(1, c)
+        stage(v_mx, 0, HALF, "w1_grouped1")
         for c in range(CHUNKS):
             weigh_on_vector(v_mx, v_factor, c)
             if c % 2 == 0:

@@ -48,15 +48,17 @@ def tile_picked_ykfac_relu_p_kernel(tc, x_words, x_scales, w1, wgt, inv, old, of
                 w_raw[g, c] = raw[:, :, columns(c - first, c - first + 1)]
 
         pass0 = keep.tile([P, PACK, N], F32, name="pass0")
-        nc.sync.dma_start(pass0[:], w_view[0])
+        all_words = [keep.tile([P, T], I32, name=f"all_words{g}", align_bytes=64) for g in range(PASSES)]
+        nc.sync.dma_start(all_words[0][:], x_words[0].rearrange("p n r -> p (n r)").bitcast(I32))
         load_weights(1, 0, 1, nc.scalar)
         for q in range(P // QUADRANT):
             rows = slice(QUADRANT * q, QUADRANT * q + PACK * PASSES)
             nc.sync.dma_start(all_scales[rows, :].bitcast(I32), x_scales[:, PACK * q : PACK * (q + 1), :].bitcast(I32))
-        all_words = [keep.tile([P, T], I32, name=f"all_words{g}", align_bytes=64) for g in range(PASSES)]
         wgt_sb = keep.tile([P, PACK], F32, name="wgt_sb")
         inv_sb = keep.tile([P, PACK], F32, name="inv_sb")
-        nc.sync.dma_start(all_words[0][:], x_words[0].rearrange("p n r -> p (n r)").bitcast(I32))
+        nc.sync.dma_start(pass0[:], w_view[0])
+        for c in range(CHUNKS):
+            w_raw[0, c] = pass0[:, :, columns(c, c + 1)]
         nc.sync.dma_start(wgt_sb[:], wgt.rearrange("(p j) o -> p (j o)", j=PACK))
         nc.sync.dma_start(inv_sb[:], inv.rearrange("(p j) o -> p (j o)", j=PACK))
         nc.sync.dma_start(all_words[1][:], x_words[1].rearrange("p n r -> p (n r)").bitcast(I32))
@@ -105,10 +107,6 @@ def tile_picked_ykfac_relu_p_kernel(tc, x_words, x_scales, w1, wgt, inv, old, of
 
         def cast(copy, g, c):
             interleave(copy, staged(w_mx[g], c, c + 1), w_raw[g, c])
-
-        def cast_half(copy, first):
-            cols = columns(first, first + HALF)
-            interleave(copy, staged(w_mx[0], first, first + HALF), pass0[:, :, cols])
 
         def quantize(mx, first, last):
             codes, scales = mx[1:]
@@ -175,13 +173,11 @@ def tile_picked_ykfac_relu_p_kernel(tc, x_words, x_scales, w1, wgt, inv, old, of
             stage(w_mx[1], c, c + 1, f"w1_grouped{c}")
         stage(a_mx, 0, CHUNKS, "a_grouped")
         stage(v_mx, HALF, CHUNKS, "v_late")
-        cast_half(on_vector, 0)
-        cast_half(on_scalar, HALF)
-        gather_scales()
-        quantize(w_mx[0], 0, HALF)
-        quantize(w_mx[0], HALF, CHUNKS)
         gather_words(0)
+        gather_scales()
         for c in range(CHUNKS):
+            cast(on_vector if c == 0 else on_scalar, 0, c)
+            quantize(w_mx[0], c, c + 1)
             first_product(0, c)
         gather_words(1)
         for c in range(CHUNKS):

@@ -22,12 +22,14 @@ PASSES = K // (P * PACK)
 CHUNKS = N // P
 HALF = CHUNKS // 2
 ROWS = (1, 0, 3, 2)
+BLOCK = 4 * N
 
 
 def tile_picked_ykfac_relu_p_kernel(tc, x_words, x_scales, w1, wgt, inv, old, offs, out):
     nc = tc.nc
     with ExitStack() as ctx:
         keep = ctx.enter_context(tc.tile_pool(name="keep", bufs=1))
+        shared = ctx.enter_context(tc.tile_pool(name="shared", bufs=1))
         psum = ctx.enter_context(tc.psum_pool(name="psum", bufs=1))
 
         def columns(first, last):
@@ -41,32 +43,26 @@ def tile_picked_ykfac_relu_p_kernel(tc, x_words, x_scales, w1, wgt, inv, old, of
         w_view = w1.rearrange("(g p j) m -> g p j m", g=PASSES, j=PACK)
         w_raw = {}
 
-        def load_weights(g, first, last, queue=nc.sync):
-            raw = keep.tile([P, PACK, (last - first) * P], F32, name=f"w_raw{g}{first}")
+        def load_weights(g, first, last, queue=nc.sync, offset=None):
+            pool = keep if offset is None else shared
+            raw = pool.tile([P, PACK, (last - first) * P], F32, name=f"w_raw{g}{first}", offset=offset)
             queue.dma_start(raw[:], w_view[g][:, :, columns(first, last)])
             for c in range(first, last):
                 w_raw[g, c] = raw[:, :, columns(c - first, c - first + 1)]
 
-        pass0 = keep.tile([P, PACK, N], F32, name="pass0")
-        all_words = [keep.tile([P, T], I32, name=f"all_words{g}", align_bytes=64) for g in range(PASSES)]
+        pass0 = shared.tile([P, PACK, N], F32, name="pass0", offset=4 * BLOCK)
+        all_words = [shared.tile([P, T], I32, name="all_words0", offset=0, align_bytes=64), keep.tile([P, T], I32, name="all_words1", align_bytes=64)]
         nc.sync.dma_start(all_words[0][:], x_words[0].rearrange("p n r -> p (n r)").bitcast(I32))
         load_weights(1, 0, 1, nc.scalar)
-        for q in range(P // QUADRANT):
-            rows = slice(QUADRANT * q, QUADRANT * q + PACK * PASSES)
-            nc.sync.dma_start(all_scales[rows, :].bitcast(I32), x_scales[:, PACK * q : PACK * (q + 1), :].bitcast(I32))
+        nc.sync.dma_start(all_scales[0:P:PACK, :].bitcast(I32), x_scales.rearrange("g i n -> i g n").bitcast(I32))
         wgt_sb = keep.tile([P, PACK], F32, name="wgt_sb")
         inv_sb = keep.tile([P, PACK], F32, name="inv_sb")
+        nc.sync.dma_start(wgt_sb[:], wgt.rearrange("(p j) o -> p (j o)", j=PACK))
+        nc.sync.dma_start(inv_sb[:], inv.rearrange("(p j) o -> p (j o)", j=PACK))
         nc.sync.dma_start(pass0[:], w_view[0])
         for c in range(CHUNKS):
             w_raw[0, c] = pass0[:, :, columns(c, c + 1)]
-        nc.sync.dma_start(wgt_sb[:], wgt.rearrange("(p j) o -> p (j o)", j=PACK))
-        nc.sync.dma_start(inv_sb[:], inv.rearrange("(p j) o -> p (j o)", j=PACK))
         nc.sync.dma_start(all_words[1][:], x_words[1].rearrange("p n r -> p (n r)").bitcast(I32))
-        for c in range(1, CHUNKS):
-            load_weights(1, c, c + 1)
-        old_sb = [keep.tile([P, N], F32, name=f"old_sb{i}") for i in range(CHUNKS)]
-        for i in ROWS:
-            nc.sync.dma_start(old_sb[i][:], old[columns(i, i + 1), :])
 
         a_factor = keep.tile([P, 1, PACK], F32, name="a_factor")
         wgt_sign = keep.tile([P, PACK], F32, name="wgt_sign")
@@ -77,14 +73,15 @@ def tile_picked_ykfac_relu_p_kernel(tc, x_words, x_scales, w1, wgt, inv, old, of
 
         def operand(name):
             grouped = {}
-            codes = keep.tile([P, N], U32, name="all_scales" if name == "w0" else f"{name}_codes", align_bytes=64)
+            codes = keep.tile([P, N], U32, name=f"{name}_codes", align_bytes=64)
             scales = keep.tile([P, N], U8, name=f"{name}_scales", align_bytes=64)
             return grouped, codes, scales
 
         w_mx = [operand(f"w{g}") for g in range(PASSES)]
         a_mx = operand("a")
         v_mx = operand("v")
-        x_codes = [keep.tile([P, S], U32, name=f"x_codes{g}", align_bytes=64) for g in range(PASSES)]
+        x_codes = {}
+        picked_scales = keep.tile([P, S], U8, name="picked_scales", align_bytes=64)
         x_planes = keep.tile([P, S], U8, name="x_planes", align_bytes=64)
         y = [psum.tile([P, PACK, P], F32, name=f"y{c}") for c in range(CHUNKS)]
         a_rows = {}
@@ -114,9 +111,14 @@ def tile_picked_ykfac_relu_p_kernel(tc, x_words, x_scales, w1, wgt, inv, old, of
             nc.vector.quantize_mx(codes[:, cols].bitcast(FP8X4), scales[:, cols], staged(mx, first, last).rearrange("p m j -> p (m j)"))
 
         def gather_scales():
-            nc.vector.tensor_copy(x_planes[:].rearrange("p (j m) -> p m j", j=PACK), all_scales[:].indirect(offsets[:]))
+            nc.vector.tensor_copy(picked_scales[:].rearrange("p (j m) -> p m j", j=PACK), all_scales[:].indirect(offsets[:]))
+            nc.vector.tensor_copy(x_planes[:].bitcast(I32), picked_scales[:].bitcast(I32))
+            for r in range(1, PACK):
+                for g in range(PASSES):
+                    nc.scalar.dma_start(x_planes[PACK * g + r : P : QUADRANT, :].bitcast(I32), picked_scales[8 * r + PACK * g : P : QUADRANT, :].bitcast(I32))
 
         def gather_words(g):
+            x_codes[g] = keep.tile([P, S], U32, name="all_scales" if g == 0 else "w0_grouped", align_bytes=64)
             nc.vector.tensor_copy(x_codes[g][:].rearrange("p (j m) -> p m j", j=PACK), all_words[g][:].bitcast(U32).indirect(offsets[:]))
 
         def first_product(g, c):
@@ -137,7 +139,7 @@ def tile_picked_ykfac_relu_p_kernel(tc, x_words, x_scales, w1, wgt, inv, old, of
             )
 
         def weigh_a_rows(c):
-            a_rows[c] = keep.tile([P, PACK, P], BF16, name="w_raw12" if c == 0 else f"a_rows{c}")
+            a_rows[c] = shared.tile([P, PACK, P], BF16, name="a_rows0", offset=BLOCK) if c == 0 else keep.tile([P, PACK, P], BF16, name=f"a_rows{c}")
             for j in range(PACK):
                 nc.scalar.activation(a_rows[c][:, j, :], y[c][:, j, :], ACT.Relu, scale=a_factor[:, 0, j : j + 1])
 
@@ -173,12 +175,18 @@ def tile_picked_ykfac_relu_p_kernel(tc, x_words, x_scales, w1, wgt, inv, old, of
             stage(w_mx[1], c, c + 1, f"w1_grouped{c}")
         stage(a_mx, 0, CHUNKS, "a_grouped")
         stage(v_mx, HALF, CHUNKS, "v_late")
-        gather_words(0)
         gather_scales()
+        gather_words(0)
+        for c in range(1, CHUNKS):
+            load_weights(1, c, c + 1, offset=(c - 1) * BLOCK)
         for c in range(CHUNKS):
             cast(on_vector if c == 0 else on_scalar, 0, c)
             quantize(w_mx[0], c, c + 1)
             first_product(0, c)
+        old_sb = {}
+        for n, i in enumerate(ROWS):
+            old_sb[i] = shared.tile([P, N], F32, name=f"old_sb{i}", offset=(3 + n) * BLOCK)
+            nc.sync.dma_start(old_sb[i][:], old[columns(i, i + 1), :])
         gather_words(1)
         for c in range(CHUNKS):
             cast(on_scalar, 1, c)

@@ -23,6 +23,9 @@ CHUNKS = N // P
 HALF = CHUNKS // 2
 ROWS = (1, 0, 3, 2)
 BLOCK = 4 * N
+PICKED = 7 * BLOCK
+STAGE = 9 * BLOCK
+WORDS1 = 11 * BLOCK
 
 
 def tile_picked_ykfac_relu_p_kernel(tc, x_words, x_scales, w1, wgt, inv, old, offs, out):
@@ -37,7 +40,7 @@ def tile_picked_ykfac_relu_p_kernel(tc, x_words, x_scales, w1, wgt, inv, old, of
 
         offsets = keep.tile([P, S // 16], U16, name="offsets")
         nc.sync.dma_start(offsets[:], offs)
-        all_scales = keep.tile([P, T], U8, name="all_scales", align_bytes=64)
+        all_scales = shared.tile([P, T], U8, name="all_scales", offset=STAGE, align_bytes=64)
         nc.vector.memset(all_scales[:].bitcast(I32), 0)
 
         w_view = w1.rearrange("(g p j) m -> g p j m", g=PASSES, j=PACK)
@@ -50,26 +53,18 @@ def tile_picked_ykfac_relu_p_kernel(tc, x_words, x_scales, w1, wgt, inv, old, of
             for c in range(first, last):
                 w_raw[g, c] = raw[:, :, columns(c - first, c - first + 1)]
 
-        pass0 = shared.tile([P, PACK, N], F32, name="pass0", offset=4 * BLOCK)
-        all_words = [shared.tile([P, T], I32, name="all_words0", offset=0, align_bytes=64), keep.tile([P, T], I32, name="all_words1", align_bytes=64)]
+        pass0 = shared.tile([P, PACK, N], F32, name="pass0", offset=BLOCK)
+        all_words = [keep.tile([P, T], I32, name="all_words0", align_bytes=64)]
         nc.sync.dma_start(all_words[0][:], x_words[0].rearrange("p n r -> p (n r)").bitcast(I32))
-        load_weights(1, 0, 1, nc.scalar)
         nc.sync.dma_start(all_scales[0:P:PACK, :].bitcast(I32), x_scales.rearrange("g i n -> i g n").bitcast(I32))
-        wgt_sb = keep.tile([P, PACK], F32, name="wgt_sb")
-        inv_sb = keep.tile([P, PACK], F32, name="inv_sb")
+        wgt_sb = keep.tile([P, PACK], F32, name="wgt_sb", align_bytes=64)
+        inv_sb = shared.tile([P, PACK], F32, name="inv_sb", offset=WORDS1)
         nc.sync.dma_start(wgt_sb[:], wgt.rearrange("(p j) o -> p (j o)", j=PACK))
         nc.sync.dma_start(inv_sb[:], inv.rearrange("(p j) o -> p (j o)", j=PACK))
+        load_weights(1, 0, 1)
         nc.sync.dma_start(pass0[:], w_view[0])
         for c in range(CHUNKS):
             w_raw[0, c] = pass0[:, :, columns(c, c + 1)]
-        nc.sync.dma_start(all_words[1][:], x_words[1].rearrange("p n r -> p (n r)").bitcast(I32))
-
-        a_factor = keep.tile([P, 1, PACK], F32, name="a_factor")
-        wgt_sign = keep.tile([P, PACK], F32, name="wgt_sign")
-        v_factor = keep.tile([P, 1, PACK], F32, name="v_factor")
-        nc.scalar.activation(a_factor[:, 0, :], wgt_sb[:], ACT.Abs)
-        nc.scalar.activation(wgt_sign[:], wgt_sb[:], ACT.Sign)
-        nc.vector.tensor_tensor(v_factor[:, 0, :], inv_sb[:], wgt_sign[:], ALU.mult)
 
         def operand(name):
             grouped = {}
@@ -81,8 +76,7 @@ def tile_picked_ykfac_relu_p_kernel(tc, x_words, x_scales, w1, wgt, inv, old, of
         a_mx = operand("a")
         v_mx = operand("v")
         x_codes = {}
-        picked_scales = keep.tile([P, S], U8, name="picked_scales", align_bytes=64)
-        x_planes = keep.tile([P, S], U8, name="x_planes", align_bytes=64)
+        picked_scales = shared.tile([P, S], U8, name="picked_scales", offset=PICKED, align_bytes=64)
         y = [psum.tile([P, PACK, P], F32, name=f"y{c}") for c in range(CHUNKS)]
         a_rows = {}
         result = keep.tile([P, CHUNKS, N], F32, name="result")
@@ -110,7 +104,7 @@ def tile_picked_ykfac_relu_p_kernel(tc, x_words, x_scales, w1, wgt, inv, old, of
             cols = columns(first, last)
             nc.vector.quantize_mx(codes[:, cols].bitcast(FP8X4), scales[:, cols], staged(mx, first, last).rearrange("p m j -> p (m j)"))
 
-        def gather_scales():
+        def gather_scales(x_planes):
             nc.vector.tensor_copy(picked_scales[:].rearrange("p (j m) -> p m j", j=PACK), all_scales[:].indirect(offsets[:]))
             nc.vector.tensor_copy(x_planes[:].bitcast(I32), picked_scales[:].bitcast(I32))
             for r in range(1, PACK):
@@ -118,7 +112,7 @@ def tile_picked_ykfac_relu_p_kernel(tc, x_words, x_scales, w1, wgt, inv, old, of
                     nc.scalar.dma_start(x_planes[PACK * g + r : P : QUADRANT, :].bitcast(I32), picked_scales[8 * r + PACK * g : P : QUADRANT, :].bitcast(I32))
 
         def gather_words(g):
-            x_codes[g] = keep.tile([P, S], U32, name="all_scales" if g == 0 else "w0_grouped", align_bytes=64)
+            x_codes[g] = shared.tile([P, S], U32, name="x_codes0", offset=STAGE + BLOCK, align_bytes=64) if g == 0 else keep.tile([P, S], U32, name="w0_grouped", align_bytes=64)
             nc.vector.tensor_copy(x_codes[g][:].rearrange("p (j m) -> p m j", j=PACK), all_words[g][:].bitcast(U32).indirect(offsets[:]))
 
         def first_product(g, c):
@@ -139,7 +133,7 @@ def tile_picked_ykfac_relu_p_kernel(tc, x_words, x_scales, w1, wgt, inv, old, of
             )
 
         def weigh_a_rows(c):
-            a_rows[c] = shared.tile([P, PACK, P], BF16, name="a_rows0", offset=BLOCK) if c == 0 else keep.tile([P, PACK, P], BF16, name=f"a_rows{c}")
+            a_rows[c] = shared.tile([P, PACK, P], BF16, name="a_rows0", offset=PICKED + S // 2) if c == 0 else keep.tile([P, PACK, P], BF16, name=f"a_rows{c}")
             for j in range(PACK):
                 nc.scalar.activation(a_rows[c][:, j, :], y[c][:, j, :], ACT.Relu, scale=a_factor[:, 0, j : j + 1])
 
@@ -175,17 +169,27 @@ def tile_picked_ykfac_relu_p_kernel(tc, x_words, x_scales, w1, wgt, inv, old, of
             stage(w_mx[1], c, c + 1, f"w1_grouped{c}")
         stage(a_mx, 0, CHUNKS, "a_grouped")
         stage(v_mx, HALF, CHUNKS, "v_late")
-        gather_scales()
+        a_factor = keep.tile([P, 1, PACK], F32, name="a_factor")
+        wgt_sign = shared.tile([P, PACK], F32, name="wgt_sign", offset=STAGE + BLOCK)
+        nc.scalar.activation(a_factor[:, 0, :], wgt_sb[:], ACT.Abs)
+        nc.scalar.activation(wgt_sign[:], wgt_sb[:], ACT.Sign)
+        x_planes = keep.tile([P, S], U8, name="wgt_sb", align_bytes=64)
+        gather_scales(x_planes)
+        v_factor = shared.tile([P, 1, PACK], F32, name="v_factor", offset=STAGE)
+        nc.vector.tensor_tensor(v_factor[:, 0, :], inv_sb[:], wgt_sign[:], ALU.mult)
         gather_words(0)
-        for c in range(1, CHUNKS):
-            load_weights(1, c, c + 1, offset=(c - 1) * BLOCK)
+        all_words.append(shared.tile([P, T], I32, name="all_words1", offset=WORDS1, align_bytes=64))
+        nc.sync.dma_start(all_words[1][:], x_words[1].rearrange("p n r -> p (n r)").bitcast(I32))
+        for c in (1, 2):
+            load_weights(1, c, c + 1, offset=PICKED + S // 2 + (c - 2) * BLOCK)
         for c in range(CHUNKS):
             cast(on_vector if c == 0 else on_scalar, 0, c)
             quantize(w_mx[0], c, c + 1)
             first_product(0, c)
+        load_weights(1, 3, 4, offset=BLOCK // 2)
         old_sb = {}
         for n, i in enumerate(ROWS):
-            old_sb[i] = shared.tile([P, N], F32, name=f"old_sb{i}", offset=(3 + n) * BLOCK)
+            old_sb[i] = shared.tile([P, N], F32, name=f"old_sb{i}", offset=BLOCK // 2 + (n + 1) * BLOCK)
             nc.sync.dma_start(old_sb[i][:], old[columns(i, i + 1), :])
         gather_words(1)
         for c in range(CHUNKS):

@@ -23,9 +23,10 @@ CHUNKS = N // P
 HALF = CHUNKS // 2
 ROWS = (1, 0, 3, 2)
 BLOCK = 4 * N
-PICKED = 7 * BLOCK
-STAGE = 9 * BLOCK
-WORDS1 = 11 * BLOCK
+WORDS0 = 0
+PASS0 = 4 * BLOCK
+STAGE = 8 * BLOCK
+WORDS1 = 10 * BLOCK
 
 
 def tile_picked_ykfac_relu_p_kernel(tc, x_words, x_scales, w1, wgt, inv, old, offs, out):
@@ -39,7 +40,6 @@ def tile_picked_ykfac_relu_p_kernel(tc, x_words, x_scales, w1, wgt, inv, old, of
             return slice(first * P, last * P)
 
         offsets = keep.tile([P, S // 16], U16, name="offsets")
-        nc.sync.dma_start(offsets[:], offs)
         all_scales = shared.tile([P, T], U8, name="all_scales", offset=STAGE, align_bytes=64)
         nc.vector.memset(all_scales[:].bitcast(I32), 0)
 
@@ -53,15 +53,16 @@ def tile_picked_ykfac_relu_p_kernel(tc, x_words, x_scales, w1, wgt, inv, old, of
             for c in range(first, last):
                 w_raw[g, c] = raw[:, :, columns(c - first, c - first + 1)]
 
-        pass0 = shared.tile([P, PACK, N], F32, name="pass0", offset=BLOCK)
-        all_words = [keep.tile([P, T], I32, name="all_words0", align_bytes=64)]
-        nc.sync.dma_start(all_words[0][:], x_words[0].rearrange("p n r -> p (n r)").bitcast(I32))
-        nc.sync.dma_start(all_scales[0:P:PACK, :].bitcast(I32), x_scales.rearrange("g i n -> i g n").bitcast(I32))
-        wgt_sb = keep.tile([P, PACK], F32, name="wgt_sb", align_bytes=64)
+        pass0 = shared.tile([P, PACK, N], F32, name="pass0", offset=PASS0)
+        all_words = [shared.tile([P, T], I32, name="all_words0", offset=WORDS0, align_bytes=64)]
+        wgt_sb = keep.tile([P, PACK], F32, name="wgt_sb")
         inv_sb = shared.tile([P, PACK], F32, name="inv_sb", offset=WORDS1)
+        nc.sync.dma_start(offsets[:], offs)
+        load_weights(1, 0, 1, nc.scalar)
         nc.sync.dma_start(wgt_sb[:], wgt.rearrange("(p j) o -> p (j o)", j=PACK))
         nc.sync.dma_start(inv_sb[:], inv.rearrange("(p j) o -> p (j o)", j=PACK))
-        load_weights(1, 0, 1)
+        nc.sync.dma_start(all_scales[0:P:PACK, :].bitcast(I32), x_scales.rearrange("g i n -> i g n").bitcast(I32))
+        nc.sync.dma_start(all_words[0][:], x_words[0].rearrange("p n r -> p (n r)").bitcast(I32))
         nc.sync.dma_start(pass0[:], w_view[0])
         for c in range(CHUNKS):
             w_raw[0, c] = pass0[:, :, columns(c, c + 1)]
@@ -76,7 +77,7 @@ def tile_picked_ykfac_relu_p_kernel(tc, x_words, x_scales, w1, wgt, inv, old, of
         a_mx = operand("a")
         v_mx = operand("v")
         x_codes = {}
-        picked_scales = shared.tile([P, S], U8, name="picked_scales", offset=PICKED, align_bytes=64)
+        picked_scales = keep.tile([P, S], U8, name="picked_scales", align_bytes=64)
         y = [psum.tile([P, PACK, P], F32, name=f"y{c}") for c in range(CHUNKS)]
         a_rows = {}
         result = keep.tile([P, CHUNKS, N], F32, name="result")
@@ -109,10 +110,10 @@ def tile_picked_ykfac_relu_p_kernel(tc, x_words, x_scales, w1, wgt, inv, old, of
             nc.vector.tensor_copy(x_planes[:].bitcast(I32), picked_scales[:].bitcast(I32))
             for r in range(1, PACK):
                 for g in range(PASSES):
-                    nc.scalar.dma_start(x_planes[PACK * g + r : P : QUADRANT, :].bitcast(I32), picked_scales[8 * r + PACK * g : P : QUADRANT, :].bitcast(I32))
+                    nc.sync.dma_start(x_planes[PACK * g + r : P : QUADRANT, :].bitcast(I32), picked_scales[8 * r + PACK * g : P : QUADRANT, :].bitcast(I32))
 
         def gather_words(g):
-            x_codes[g] = shared.tile([P, S], U32, name="x_codes0", offset=STAGE + BLOCK, align_bytes=64) if g == 0 else keep.tile([P, S], U32, name="w0_grouped", align_bytes=64)
+            x_codes[g] = keep.tile([P, S], U32, name="x_codes0" if g == 0 else "w0_grouped", align_bytes=64)
             nc.vector.tensor_copy(x_codes[g][:].rearrange("p (j m) -> p m j", j=PACK), all_words[g][:].bitcast(U32).indirect(offsets[:]))
 
         def first_product(g, c):
@@ -133,7 +134,7 @@ def tile_picked_ykfac_relu_p_kernel(tc, x_words, x_scales, w1, wgt, inv, old, of
             )
 
         def weigh_a_rows(c):
-            a_rows[c] = shared.tile([P, PACK, P], BF16, name="a_rows0", offset=PICKED + S // 2) if c == 0 else keep.tile([P, PACK, P], BF16, name=f"a_rows{c}")
+            a_rows[c] = shared.tile([P, PACK, P], BF16, name="a_rows0", offset=WORDS0 + BLOCK) if c == 0 else keep.tile([P, PACK, P], BF16, name=f"a_rows{c}")
             for j in range(PACK):
                 nc.scalar.activation(a_rows[c][:, j, :], y[c][:, j, :], ACT.Relu, scale=a_factor[:, 0, j : j + 1])
 
@@ -169,27 +170,26 @@ def tile_picked_ykfac_relu_p_kernel(tc, x_words, x_scales, w1, wgt, inv, old, of
             stage(w_mx[1], c, c + 1, f"w1_grouped{c}")
         stage(a_mx, 0, CHUNKS, "a_grouped")
         stage(v_mx, HALF, CHUNKS, "v_late")
-        a_factor = keep.tile([P, 1, PACK], F32, name="a_factor")
-        wgt_sign = shared.tile([P, PACK], F32, name="wgt_sign", offset=STAGE + BLOCK)
-        nc.scalar.activation(a_factor[:, 0, :], wgt_sb[:], ACT.Abs)
+        wgt_sign = keep.tile([P, PACK], F32, name="wgt_sign")
         nc.scalar.activation(wgt_sign[:], wgt_sb[:], ACT.Sign)
-        x_planes = keep.tile([P, S], U8, name="wgt_sb", align_bytes=64)
+        x_planes = keep.tile([P, S], U8, name="x_planes", align_bytes=64)
         gather_scales(x_planes)
         v_factor = shared.tile([P, 1, PACK], F32, name="v_factor", offset=STAGE)
         nc.vector.tensor_tensor(v_factor[:, 0, :], inv_sb[:], wgt_sign[:], ALU.mult)
+        a_factor = keep.tile([P, 1, PACK], F32, name="a_factor")
+        nc.scalar.activation(a_factor[:, 0, :], wgt_sb[:], ACT.Abs)
         gather_words(0)
         all_words.append(shared.tile([P, T], I32, name="all_words1", offset=WORDS1, align_bytes=64))
         nc.sync.dma_start(all_words[1][:], x_words[1].rearrange("p n r -> p (n r)").bitcast(I32))
-        for c in (1, 2):
-            load_weights(1, c, c + 1, offset=PICKED + S // 2 + (c - 2) * BLOCK)
+        for c in range(1, CHUNKS):
+            load_weights(1, c, c + 1, offset=WORDS0 + (c - 1) * BLOCK)
         for c in range(CHUNKS):
             cast(on_vector if c == 0 else on_scalar, 0, c)
             quantize(w_mx[0], c, c + 1)
             first_product(0, c)
-        load_weights(1, 3, 4, offset=BLOCK // 2)
         old_sb = {}
         for n, i in enumerate(ROWS):
-            old_sb[i] = shared.tile([P, N], F32, name=f"old_sb{i}", offset=BLOCK // 2 + (n + 1) * BLOCK)
+            old_sb[i] = shared.tile([P, N], F32, name=f"old_sb{i}", offset=PASS0 + (n - 1) * BLOCK)
             nc.sync.dma_start(old_sb[i][:], old[columns(i, i + 1), :])
         gather_words(1)
         for c in range(CHUNKS):

@@ -105,12 +105,13 @@ def tile_picked_ykfac_relu_p_kernel(tc, x_words, x_scales, w1, wgt, inv, old, of
             cols = columns(first, last)
             nc.vector.quantize_mx(codes[:, cols].bitcast(FP8X4), scales[:, cols], staged(mx, first, last).rearrange("p m j -> p (m j)"))
 
-        def gather_scales(x_planes):
+        def gather_scales():
             nc.vector.tensor_copy(picked_scales[:].rearrange("p (j m) -> p m j", j=PACK), all_scales[:].indirect(offsets[:]))
-            nc.vector.tensor_copy(x_planes[:].bitcast(I32), picked_scales[:].bitcast(I32))
+
+        def place_scales(g, queue):
+            nc.vector.tensor_copy(x_planes[g][:].bitcast(I32), picked_scales[:].bitcast(I32))
             for r in range(1, PACK):
-                for g in range(PASSES):
-                    nc.sync.dma_start(x_planes[PACK * g + r : P : QUADRANT, :].bitcast(I32), picked_scales[8 * r + PACK * g : P : QUADRANT, :].bitcast(I32))
+                queue.dma_start(x_planes[g][PACK * g + r : P : QUADRANT, :].bitcast(I32), picked_scales[8 * r + PACK * g : P : QUADRANT, :].bitcast(I32))
 
         def gather_words(g):
             x_codes[g] = keep.tile([P, S], U32, name="x_codes0" if g == 0 else "w0_grouped", align_bytes=64)
@@ -121,7 +122,7 @@ def tile_picked_ykfac_relu_p_kernel(tc, x_words, x_scales, w1, wgt, inv, old, of
                 nc.tensor.matmul_mx(
                     out=y[c][:, j, :],
                     lhsT=x_codes[g][:, columns(j, j + 1)].bitcast(FP8X4),
-                    lhsT_scale=x_planes[PACK * g : P, columns(j, j + 1)],
+                    lhsT_scale=x_planes[g][PACK * g : P, columns(j, j + 1)],
                     rhs=w_mx[g][1][:, columns(c, c + 1)].bitcast(FP8X4),
                     rhs_scale=w_mx[g][2][:, columns(c, c + 1)],
                     start=(g == 0 and j == 0),
@@ -172,15 +173,17 @@ def tile_picked_ykfac_relu_p_kernel(tc, x_words, x_scales, w1, wgt, inv, old, of
         stage(v_mx, HALF, CHUNKS, "v_late")
         wgt_sign = keep.tile([P, PACK], F32, name="wgt_sign")
         nc.scalar.activation(wgt_sign[:], wgt_sb[:], ACT.Sign)
-        x_planes = keep.tile([P, S], U8, name="x_planes", align_bytes=64)
-        gather_scales(x_planes)
+        x_planes = [keep.tile([P, S], U8, name=f"x_planes{g}", align_bytes=64) for g in range(PASSES)]
+        gather_scales()
+        place_scales(0, nc.sync)
         v_factor = shared.tile([P, 1, PACK], F32, name="v_factor", offset=STAGE)
         nc.vector.tensor_tensor(v_factor[:, 0, :], inv_sb[:], wgt_sign[:], ALU.mult)
         a_factor = keep.tile([P, 1, PACK], F32, name="a_factor")
         nc.scalar.activation(a_factor[:, 0, :], wgt_sb[:], ACT.Abs)
-        gather_words(0)
         all_words.append(shared.tile([P, T], I32, name="all_words1", offset=WORDS1, align_bytes=64))
         nc.sync.dma_start(all_words[1][:], x_words[1].rearrange("p n r -> p (n r)").bitcast(I32))
+        place_scales(1, nc.scalar)
+        gather_words(0)
         for c in range(1, CHUNKS):
             load_weights(1, c, c + 1, offset=WORDS0 + (c - 1) * BLOCK)
         for c in range(CHUNKS):

@@ -22,6 +22,7 @@ PASSES = K // (P * PACK)
 CHUNKS = N // P
 HALF = CHUNKS // 2
 ROWS = (1, 0, 3, 2)
+RUN = 8
 BLOCK = 4 * N
 WORDS0 = 0
 PASS0 = 4 * BLOCK
@@ -41,6 +42,8 @@ def tile_picked_ykfac_relu_p_kernel(tc, x_words, x_scales, w1, wgt, inv, old, of
 
         offsets = keep.tile([P, S // 16], U16, name="offsets")
         all_scales = shared.tile([P, T], U8, name="all_scales", offset=STAGE, align_bytes=64)
+        factor_rows = shared.tile([P, 2, QUADRANT], F32, name="factor_rows", offset=WORDS1, align_bytes=64)
+        nc.vector.memset(factor_rows[:], 0.0)
         nc.vector.memset(all_scales[:].bitcast(I32), 0)
 
         w_view = w1.rearrange("(g p j) m -> g p j m", g=PASSES, j=PACK)
@@ -55,12 +58,11 @@ def tile_picked_ykfac_relu_p_kernel(tc, x_words, x_scales, w1, wgt, inv, old, of
 
         pass0 = shared.tile([P, PACK, N], F32, name="pass0", offset=PASS0)
         all_words = [shared.tile([P, T], I32, name="all_words0", offset=WORDS0, align_bytes=64)]
-        wgt_sb = keep.tile([P, PACK], F32, name="wgt_sb")
-        inv_sb = shared.tile([P, PACK], F32, name="inv_sb", offset=WORDS1)
         nc.sync.dma_start(offsets[:], offs)
         load_weights(1, 0, 1, nc.scalar)
-        nc.sync.dma_start(wgt_sb[:], wgt.rearrange("(p j) o -> p (j o)", j=PACK))
-        nc.sync.dma_start(inv_sb[:], inv.rearrange("(p j) o -> p (j o)", j=PACK))
+        for n, factor in enumerate((wgt, inv)):
+            rows = factor_rows[0:P:RUN, n, :].rearrange("a (x r) -> a x r", r=RUN)
+            nc.sync.dma_start(rows, factor.rearrange("(x a r) o -> a x (r o)", x=PACK, r=RUN))
         nc.sync.dma_start(all_scales[0:P:PACK, :].bitcast(I32), x_scales.rearrange("g i n -> i g n").bitcast(I32))
         nc.sync.dma_start(all_words[0][:], x_words[0].rearrange("p n r -> p (n r)").bitcast(I32))
         nc.sync.dma_start(pass0[:], w_view[0])
@@ -106,7 +108,7 @@ def tile_picked_ykfac_relu_p_kernel(tc, x_words, x_scales, w1, wgt, inv, old, of
             nc.vector.quantize_mx(codes[:, cols].bitcast(FP8X4), scales[:, cols], staged(mx, first, last).rearrange("p m j -> p (m j)"))
 
         def gather_scales():
-            nc.vector.tensor_copy(picked_scales[:].rearrange("p (j m) -> p m j", j=PACK), all_scales[:].indirect(offsets[:]))
+            nc.vector.tensor_copy(picked_scales[:].rearrange("p (j q x r) -> p x q j r", j=PACK, x=PACK, r=RUN), all_scales[:].indirect(offsets[:]))
 
         def place_scales(g, queue):
             nc.vector.tensor_copy(x_planes[g][:].bitcast(I32), picked_scales[:].bitcast(I32))
@@ -115,7 +117,7 @@ def tile_picked_ykfac_relu_p_kernel(tc, x_words, x_scales, w1, wgt, inv, old, of
 
         def gather_words(g):
             x_codes[g] = keep.tile([P, S], U32, name="x_codes0" if g == 0 else "w0_grouped", align_bytes=64)
-            nc.vector.tensor_copy(x_codes[g][:].rearrange("p (j m) -> p m j", j=PACK), all_words[g][:].bitcast(U32).indirect(offsets[:]))
+            nc.vector.tensor_copy(x_codes[g][:].rearrange("p (j q x r) -> p x q j r", j=PACK, x=PACK, r=RUN), all_words[g][:].bitcast(U32).indirect(offsets[:]))
 
         def first_product(g, c):
             for j in range(PACK):
@@ -171,18 +173,21 @@ def tile_picked_ykfac_relu_p_kernel(tc, x_words, x_scales, w1, wgt, inv, old, of
             stage(w_mx[1], c, c + 1, f"w1_grouped{c}")
         stage(a_mx, 0, CHUNKS, "a_grouped")
         stage(v_mx, HALF, CHUNKS, "v_late")
-        wgt_sign = keep.tile([P, PACK], F32, name="wgt_sign")
-        nc.scalar.activation(wgt_sign[:], wgt_sb[:], ACT.Sign)
         x_planes = [keep.tile([P, S], U8, name=f"x_planes{g}", align_bytes=64) for g in range(PASSES)]
         gather_scales()
         place_scales(0, nc.sync)
-        v_factor = shared.tile([P, 1, PACK], F32, name="v_factor", offset=STAGE)
-        nc.vector.tensor_tensor(v_factor[:, 0, :], inv_sb[:], wgt_sign[:], ALU.mult)
-        a_factor = keep.tile([P, 1, PACK], F32, name="a_factor")
-        nc.scalar.activation(a_factor[:, 0, :], wgt_sb[:], ACT.Abs)
+        factors = shared.tile([P, 2, QUADRANT], F32, name="factors", offset=STAGE, align_bytes=64)
+        for n in range(2):
+            nc.vector.transpose(factors[:, n, :], factor_rows[:, n, :])
         all_words.append(shared.tile([P, T], I32, name="all_words1", offset=WORDS1, align_bytes=64))
         nc.sync.dma_start(all_words[1][:], x_words[1].rearrange("p n r -> p (n r)").bitcast(I32))
         place_scales(1, nc.scalar)
+        a_factor = keep.tile([P, 1, PACK], F32, name="a_factor")
+        wgt_sign = keep.tile([P, PACK], F32, name="wgt_sign")
+        v_factor = keep.tile([P, 1, PACK], F32, name="v_factor")
+        nc.scalar.activation(a_factor[:, 0, :], factors[:, 0, 0:QUADRANT:RUN], ACT.Abs)
+        nc.scalar.activation(wgt_sign[:], factors[:, 0, 0:QUADRANT:RUN], ACT.Sign)
+        nc.vector.tensor_tensor(v_factor[:, 0, :], factors[:, 1, 0:QUADRANT:RUN], wgt_sign[:], ALU.mult)
         gather_words(0)
         for c in range(1, CHUNKS):
             load_weights(1, c, c + 1, offset=WORDS0 + (c - 1) * BLOCK)

@@ -205,23 +205,38 @@ def tile_picked_ykfac_relu_p_kernel(tc, x_words, x_scales, w1, wgt, inv, old, of
             quantize(w_mx[1], c, c + 1)
             first_product(1, c)
         stage(v_mx, 0, HALF, "w1_grouped1")
-        for c in range(CHUNKS):
-            weigh_on_vector(v_mx, v_factor, c)
-            if c % 2 == 0:
-                weigh_a_rows(c)
-                interleave_a(c)
-            else:
-                weigh_on_vector(a_mx, a_factor, c)
-        scale_old(ROWS, "kept")
-        quantize(v_mx, 0, HALF)
-        quantize(a_mx, ROWS[0], ROWS[0] + 1)
-        second_product("left", ROWS[0], (0, HALF))
-        quantize(v_mx, HALF, CHUNKS)
-        second_product("right", ROWS[0], (HALF, CHUNKS))
-        for i in ROWS[1:]:
-            quantize(a_mx, i, i + 1)
-            second_product(f"y{i}", i, (0, CHUNKS))
-        average(ROWS[0], (0, HALF))
-        average(ROWS[0], (HALF, CHUNKS))
-        for i in ROWS[1:]:
-            average(i, (0, CHUNKS))
+        left, right = (0, HALF), (HALF, CHUNKS)
+        weigh_on_vector(v_mx, v_factor, 0)
+        weigh_a_rows(0)
+        interleave_a(0)
+        weigh_on_vector(v_mx, v_factor, 1)
+        weigh_on_vector(a_mx, a_factor, 1)
+        scale_old((1,), "kept1")
+        weigh_on_vector(v_mx, v_factor, 2)
+        weigh_a_rows(2)
+        scale_old((0,), "kept0")
+        interleave_a(2)
+        scale_old((3, 2), "kept_late")
+        quantize(v_mx, *left)
+        quantize(a_mx, 1, 2)
+        second_product("left1", 1, left)
+        weigh_on_vector(v_mx, v_factor, 3)
+        quantize(a_mx, 0, 1)
+        second_product("left0", 0, left)
+        average(1, left)
+        quantize(v_mx, *right)
+        second_product("right1", 1, right)
+        second_product("right0", 0, right)
+        weigh_on_vector(a_mx, a_factor, 3)
+        average(0, left)
+        quantize(a_mx, 3, 4)
+        second_product("y0", 3, left)
+        second_product("y1", 3, right)
+        average(1, right)
+        average(0, right)
+        quantize(a_mx, 2, 3)
+        second_product("y3", 2, left)
+        second_product("y2", 2, right)
+        for i in ROWS[HALF:]:
+            average(i, left)
+            average(i, right)

@@ -87,8 +87,8 @@ def tile_picked_ykfac_relu_p_kernel(tc, x_words, x_scales, w1, wgt, inv, old, of
         kept = {}
         banks = {}
 
-        def stage(mx, first, last, name):
-            space = keep.tile([P, (last - first) * P, PACK], BF16, name=name, align_bytes=64)
+        def stage(mx, first, last, name, offset=None):
+            space = (keep if offset is None else shared).tile([P, (last - first) * P, PACK], BF16, name=name, align_bytes=64, offset=offset)
             for c in range(first, last):
                 mx[0][c] = (space, first)
 
@@ -204,7 +204,7 @@ def tile_picked_ykfac_relu_p_kernel(tc, x_words, x_scales, w1, wgt, inv, old, of
             cast(on_scalar, 1, c)
             quantize(w_mx[1], c, c + 1)
             first_product(1, c)
-        stage(v_mx, 0, HALF, "w1_grouped1")
+        stage(v_mx, 0, HALF, "v_early", WORDS0)
         left, right = (0, HALF), (HALF, CHUNKS)
         weigh_on_vector(v_mx, v_factor, 0)
         weigh_a_rows(0)

from contextlib import ExitStack

import concourse.mybir as mybir

K, T, S, N = 1024, 2048, 512, 512
FLOPS = 2 * S * K * N + 2 * S * N * N

F32 = mybir.dt.float32
BF16 = mybir.dt.bfloat16
I32 = mybir.dt.int32
U32 = mybir.dt.uint32
U16 = mybir.dt.uint16
U8 = mybir.dt.uint8
FP8X4 = mybir.dt.float8_e4m3fn_x4
ALU = mybir.AluOpType
ACT = mybir.ActivationFunctionType

P = 128
PACK = 4
QUADRANT = 32
PASSES = K // (P * PACK)
CHUNKS = N // P
HALF = CHUNKS // 2
ROWS = (1, 0, 3, 2)
RUN = 8
BLOCK = 4 * N
WORDS0 = 0
PASS0 = 4 * BLOCK
STAGE = 8 * BLOCK
WORDS1 = 10 * BLOCK


def tile_picked_ykfac_relu_p_kernel(tc, x_words, x_scales, w1, wgt, inv, old, offs, out):
    nc = tc.nc
    with ExitStack() as ctx:
        keep = ctx.enter_context(tc.tile_pool(name="keep", bufs=1))
        shared = ctx.enter_context(tc.tile_pool(name="shared", bufs=1))
        psum = ctx.enter_context(tc.psum_pool(name="psum", bufs=1))

        def columns(first, last):
            return slice(first * P, last * P)

        offsets = keep.tile([P, S // 16], U16, name="offsets")
        all_scales = shared.tile([P, T], U8, name="all_scales", offset=STAGE, align_bytes=64)
        factor_rows = shared.tile([P, 2, QUADRANT], F32, name="factor_rows", offset=WORDS1, align_bytes=64)
        nc.vector.memset(factor_rows[:], 0.0)
        nc.vector.memset(all_scales[:].bitcast(I32), 0)

        w_view = w1.rearrange("(g p j) m -> g p j m", g=PASSES, j=PACK)
        w_raw = {}

        def load_weights(g, first, last, queue=nc.sync, offset=None):
            pool = keep if offset is None else shared
            raw = pool.tile([P, PACK, (last - first) * P], F32, name=f"w_raw{g}{first}", offset=offset)
            queue.dma_start(raw[:], w_view[g][:, :, columns(first, last)])
            for c in range(first, last):
                w_raw[g, c] = raw[:, :, columns(c - first, c - first + 1)]

        pass0 = shared.tile([P, PACK, N], F32, name="pass0", offset=PASS0)
        all_words = [shared.tile([P, T], I32, name="all_words0", offset=WORDS0, align_bytes=64)]
        nc.sync.dma_start(offsets[:], offs)
        load_weights(1, 0, 1, nc.scalar)
        for n, factor in enumerate((wgt, inv)):
            rows = factor_rows[0:P:RUN, n, :].rearrange("a (x r) -> a x r", r=RUN)
            nc.sync.dma_start(rows, factor.rearrange("(x a r) o -> a x (r o)", x=PACK, r=RUN))
        nc.sync.dma_start(all_scales[0:P:PACK, :].bitcast(I32), x_scales.rearrange("g i n -> i g n").bitcast(I32))
        nc.sync.dma_start(all_words[0][:], x_words[0].rearrange("p n r -> p (n r)").bitcast(I32))
        nc.sync.dma_start(pass0[:], w_view[0])
        for c in range(CHUNKS):
            w_raw[0, c] = pass0[:, :, columns(c, c + 1)]

        def operand(name):
            grouped = {}
            codes = keep.tile([P, N], U32, name=f"{name}_codes", align_bytes=64)
            scales = keep.tile([P, N], U8, name=f"{name}_scales", align_bytes=64)
            return grouped, codes, scales

        w_mx = [operand(f"w{g}") for g in range(PASSES)]
        a_mx = operand("a")
        v_mx = operand("v")
        x_codes = {}
        picked_scales = keep.tile([P, S], U8, name="picked_scales", align_bytes=64)
        y = [psum.tile([P, PACK, P], F32, name=f"y{c}") for c in range(CHUNKS)]
        a_rows = {}
        result = keep.tile([P, CHUNKS, N], F32, name="result")
        out_rows = out.rearrange("(i p) m -> p i m", p=P)
        kept = {}
        banks = {}

        def stage(mx, first, last, name, offset=None):
            space = (keep if offset is None else shared).tile([P, (last - first) * P, PACK], BF16, name=name, align_bytes=64, offset=offset)
            for c in range(first, last):
                mx[0][c] = (space, first)

        def staged(mx, first, last):
            space, start = mx[0][first]
            return space[:, columns(first - start, last - start)]

        def interleave(copy, grouped, rows):
            copy(grouped.rearrange("p (u i) j -> p u j i", i=4), rows.rearrange("p j (u i) -> p u j i", i=4))

        def cast(copy, g, c):
            interleave(copy, staged(w_mx[g], c, c + 1), w_raw[g, c])

        def quantize(mx, first, last):
            codes, scales = mx[1:]
            cols = columns(first, last)
            nc.vector.quantize_mx(codes[:, cols].bitcast(FP8X4), scales[:, cols], staged(mx, first, last).rearrange("p m j -> p (m j)"))

        def gather_scales():
            nc.vector.tensor_copy(picked_scales[:].rearrange("p (j q x r) -> p x q j r", j=PACK, x=PACK, r=RUN), all_scales[:].indirect(offsets[:]))

        def place_scales(g, queue):
            nc.vector.tensor_copy(x_planes[g][:].bitcast(I32), picked_scales[:].bitcast(I32))
            for r in range(1, PACK):
                queue.dma_start(x_planes[g][PACK * g + r : P : QUADRANT, :].bitcast(I32), picked_scales[8 * r + PACK * g : P : QUADRANT, :].bitcast(I32))

        def gather_words(g):
            x_codes[g] = keep.tile([P, S], U32, name="x_codes0" if g == 0 else "w0_grouped", align_bytes=64)
            nc.vector.tensor_copy(x_codes[g][:].rearrange("p (j q x r) -> p x q j r", j=PACK, x=PACK, r=RUN), all_words[g][:].bitcast(U32).indirect(offsets[:]))

        def first_product(g, c):
            for j in range(PACK):
                nc.tensor.matmul_mx(
                    out=y[c][:, j, :],
                    lhsT=x_codes[g][:, columns(j, j + 1)].bitcast(FP8X4),
                    lhsT_scale=x_planes[g][PACK * g : P, columns(j, j + 1)],
                    rhs=w_mx[g][1][:, columns(c, c + 1)].bitcast(FP8X4),
                    rhs_scale=w_mx[g][2][:, columns(c, c + 1)],
                    start=(g == 0 and j == 0),
                    stop=(g == PASSES - 1 and j == PACK - 1),
                )

        def weigh_on_vector(mx, factor, c):
            nc.vector.scalar_tensor_tensor(
                staged(mx, c, c + 1), y[c][:].rearrange("p j m -> p m j"), 0.0, factor[:].to_broadcast([P, P, PACK]), ALU.max, ALU.mult
            )

        def weigh_a_rows(c):
            a_rows[c] = shared.tile([P, PACK, P], BF16, name="a_rows0", offset=WORDS0 + BLOCK) if c == 0 else keep.tile([P, PACK, P], BF16, name=f"a_rows{c}")
            for j in range(PACK):
                nc.scalar.activation(a_rows[c][:, j, :], y[c][:, j, :], ACT.Relu, scale=a_factor[:, 0, j : j + 1])

        def interleave_a(c):
            interleave(nc.scalar.copy, staged(a_mx, c, c + 1), a_rows[c][:])

        def scale_old(rows, name):
            space = keep.tile([P, len(rows), N], F32, name=name)
            for n, i in enumerate(rows):
                kept[i] = space[:, n : n + 1, :]
                nc.scalar.activation(space[:, n, :], old_sb[i][:], ACT.Copy, scale=0.95)

        def second_product(name, i, cols):
            banks[i, cols] = psum.tile([P, 1, (cols[1] - cols[0]) * P], F32, name=name)
            nc.tensor.matmul_mx(
                out=banks[i, cols][:, 0, :],
                lhsT=a_mx[1][:, columns(i, i + 1)].bitcast(FP8X4),
                lhsT_scale=a_mx[2][:, columns(i, i + 1)],
                rhs=v_mx[1][:, columns(*cols)].bitcast(FP8X4),
                rhs_scale=v_mx[2][:, columns(*cols)],
                start=True,
                stop=True,
            )

        def average(i, cols):
            part = (slice(None), slice(i, i + 1), columns(*cols))
            nc.vector.scalar_tensor_tensor(result[part], banks[i, cols][:], 0.05, kept[i][:, :, columns(*cols)], ALU.mult, ALU.add)
            nc.sync.dma_start(out_rows[part], result[part])

        on_vector, on_scalar = nc.vector.tensor_copy, nc.scalar.copy
        stage(w_mx[0], 0, CHUNKS, "w0_grouped")
        for c in range(CHUNKS):
            stage(w_mx[1], c, c + 1, f"w1_grouped{c}")
        stage(a_mx, 0, CHUNKS, "a_grouped")
        stage(v_mx, HALF, CHUNKS, "v_late")
        x_planes = [keep.tile([P, S], U8, name=f"x_planes{g}", align_bytes=64) for g in range(PASSES)]
        gather_scales()
        place_scales(0, nc.sync)
        factors = shared.tile([P, 2, QUADRANT], F32, name="factors", offset=STAGE, align_bytes=64)
        for n in range(2):
            nc.vector.transpose(factors[:, n, :], factor_rows[:, n, :])
        all_words.append(shared.tile([P, T], I32, name="all_words1", offset=WORDS1, align_bytes=64))
        nc.sync.dma_start(all_words[1][:], x_words[1].rearrange("p n r -> p (n r)").bitcast(I32))
        place_scales(1, nc.scalar)
        a_factor = keep.tile([P, 1, PACK], F32, name="a_factor")
        wgt_sign = keep.tile([P, PACK], F32, name="wgt_sign")
        v_factor = keep.tile([P, 1, PACK], F32, name="v_factor")
        nc.scalar.activation(a_factor[:, 0, :], factors[:, 0, 0:QUADRANT:RUN], ACT.Abs)
        nc.scalar.activation(wgt_sign[:], factors[:, 0, 0:QUADRANT:RUN], ACT.Sign)
        nc.vector.tensor_tensor(v_factor[:, 0, :], factors[:, 1, 0:QUADRANT:RUN], wgt_sign[:], ALU.mult)
        gather_words(0)
        for c in range(1, CHUNKS):
            load_weights(1, c, c + 1, offset=WORDS0 + (c - 1) * BLOCK)
        for c in range(CHUNKS):
            cast(on_vector if c == 0 else on_scalar, 0, c)
            quantize(w_mx[0], c, c + 1)
            first_product(0, c)
        old_sb = {}
        for n, i in enumerate(ROWS):
            old_sb[i] = shared.tile([P, N], F32, name=f"old_sb{i}", offset=PASS0 + (n - 1) * BLOCK)
            nc.sync.dma_start(old_sb[i][:], old[columns(i, i + 1), :])
        gather_words(1)
        for c in range(CHUNKS):
            cast(on_scalar, 1, c)
            quantize(w_mx[1], c, c + 1)
            first_product(1, c)
        stage(v_mx, 0, HALF, "v_early", WORDS0)
        left, right = (0, HALF), (HALF, CHUNKS)
        weigh_on_vector(v_mx, v_factor, 0)
        weigh_a_rows(0)
        interleave_a(0)
        weigh_on_vector(v_mx, v_factor, 1)
        weigh_on_vector(a_mx, a_factor, 1)
        scale_old((1,), "kept1")
        weigh_on_vector(v_mx, v_factor, 2)
        weigh_a_rows(2)
        scale_old((0,), "kept0")
        interleave_a(2)
        scale_old((3, 2), "kept_late")
        quantize(v_mx, *left)
        quantize(a_mx, 1, 2)
        second_product("left1", 1, left)
        weigh_on_vector(v_mx, v_factor, 3)
        quantize(a_mx, 0, 1)
        second_product("left0", 0, left)
        average(1, left)
        quantize(v_mx, *right)
        second_product("right1", 1, right)
        second_product("right0", 0, right)
        weigh_on_vector(a_mx, a_factor, 3)
        average(0, left)
        quantize(a_mx, 3, 4)
        second_product("y0", 3, left)
        second_product("y1", 3, right)
        average(1, right)
        average(0, right)
        quantize(a_mx, 2, 3)
        second_product("y3", 2, left)
        second_product("y2", 2, right)
        for i in ROWS[HALF:]:
            average(i, left)
            average(i, right)
